import numpy as np, ml_dtypes
CORES = [6,15,38,47]
N = 4
import mx_ref
BF = ml_dtypes.bfloat16
def gentries(a):
    return np.ascontiguousarray(a.reshape(8, 16, -1).transpose(0, 2, 1)).reshape(8, -1)
def gtable(e):
    e = np.asarray(e); return np.ascontiguousarray(e.reshape(8, -1, 16).transpose(0, 2, 1)).reshape(128, -1).astype(np.int32)
def gcols(t, e):
    v = np.concatenate([t.reshape(8, 16, -1, 4), np.zeros((8, 16, 1, 4), BF)], axis=2)
    return np.ascontiguousarray(np.stack([v[g][:, e[g]] for g in range(8)])).reshape(128, -1)
def gpick(z, e):
    return np.concatenate([z[16 * g:16 * g + 16][:, e[g]] for g in range(8)])
def tile(rs):
    return np.stack(rs, axis=2).reshape(128, -1).astype(BF)
def pick(q, e):
    c = np.concatenate([q[0].reshape(128, -1, 4), np.zeros((128, 1, 4), np.uint8)], axis=1); s = np.concatenate([q[1], np.ones((16, 1), np.uint8)], axis=1)
    return (np.ascontiguousarray(c[:, e].reshape(128, -1)), np.ascontiguousarray(s[:, e]))
def join(*qs):
    return (np.concatenate([q[0] for q in qs], axis=1), np.concatenate([q[1] for q in qs], axis=1))
def put(q, e, v):
    c, s = q[0].reshape(128, -1, 4).copy(), q[1].copy(); c[:, e] = v[0].reshape(128, -1, 4); s[:, e] = v[1]
    return (c.reshape(128, -1), s)
def pk(c, s):
    return (np.ascontiguousarray(c), mx_ref.live(s))
def emit(q):
    return q[0], q[1]
def packed(v, rng):
    q = [mx_ref.quantize(np.ascontiguousarray(v[r])) for r in range(N)]
    return np.stack([a for a, b in q]), np.stack([mx_ref.plane(b, rng) for a, b in q])
def values_of_codes():
    e, c = np.zeros((128, 128, 4), np.float32), np.zeros((128, 2, 4), np.uint8)
    e[np.arange(128), np.arange(128), 0] = 1
    c[:127, :, 0] = np.arange(256).reshape(2, 128).T[:127]
    return mx_ref.matmul(mx_ref.quantize(e.reshape(128, 512).astype(BF)), (c.reshape(128, 8), np.full((16, 2), 127, np.uint8))).T.reshape(-1).astype(np.float64)
CODE_VALUE, SCALE_VALUE = values_of_codes(), 2.0 ** (np.arange(256) - 127.0)
def decode(q):
    return (CODE_VALUE[q[0]].reshape(16, 8, -1, 4) * SCALE_VALUE[q[1]][:, None, :, None] + 0.0).reshape(128, -1).astype(np.float32)
def f(rng, *shape):
    return mx_ref.flush((rng.standard_normal(shape, dtype=np.float32) * np.exp2(rng.integers(-2, 3, shape[:-1] + (1,)))).astype(BF))
def wide(rng, *shape, cols=0):
    v = rng.standard_normal(shape, dtype=np.float32) * np.exp2(rng.integers(-12, 13, shape)).astype(np.float32)
    if cols: v *= np.repeat(np.exp2(rng.integers(-cols, cols + 1, shape[:-2] + (1, shape[-1] // 4))) * (rng.random(shape[:-2] + (1, shape[-1] // 4)) > 0.0625), 4, axis=-1).astype(np.float32)
    return mx_ref.flush(v.astype(BF))
C = 384
MASK = [1, 2, 3]
PARITY = np.array([(r ^ (r >> 1) ^ (r >> 2)) & 1 for r in range(N)])
def numbers_of(rng):
    return {"x": np.array(f(rng, N, 128, 4 * C)), "u": np.array(f(rng, N, 128, 512)), "v": np.array(f(rng, N, 128, 512))}
def stored(k):
    return {"fl": np.stack([gtable(k[r]) for r in range(N)])}
def lists(rng):
    return stored(rng.permuted(np.tile(np.arange(C), (N, 8, 1)), axis=2))
def layers(rng):
    return np.array(f(rng, N, 128, 2048)).reshape(N, 8, 16, 4, 8, 16, 4)
def weights(rng, w):
    c, p = packed(np.ascontiguousarray(w).reshape(N, 128, 2048), rng)
    return {"wc": c, "ws": p}
def setup_inputs(rng):
    return {**numbers_of(rng), **lists(rng), **weights(rng, layers(rng))}
def setup_inputs_long(rng):
    d = numbers_of(rng)
    kind = rng.permutation(8)
    s = np.tile(rng.choice([-1.0, 1.0], (8, C)), (N, 1, 1))
    k = np.zeros((N, 8, C), np.int64)
    for g in range(8):
        c, p = rng.permutation(C), int(rng.integers(C))
        if kind[g] == 0: c, p = np.arange(C), C - N // 2
        if kind[g] == 1: c = np.arange(C)[::-1]
        k[:, g, c] = np.roll(c, -1)
        for r in range(N):
            if kind[g] in (0, 1, 3, 4): s[r, g, c[(p + r) % C]] *= -1
            if kind[g] == 2 and PARITY[r]: s[r, g, c[p]] *= -1
            if kind[g] == 6 and PARITY[r]: s[r, g] *= -1
            if kind[g] == 7:
                s[r, g] = rng.choice([-1.0, 1.0], C)
                k[r, g] = np.arange(C)
    x = d["x"].reshape(N, 8, 16, C, 4)
    x[:, :, 0] = 0
    x[:, :, 0, :, 0] = s.astype(np.float32).astype(BF)
    u = d["u"].reshape(N, 128, 128, 4)
    u[:, :, ::16] = 0
    for h in range(0, 128, 16): u[:, h, h, 0] = 1
    w = layers(rng)
    w[:, :, :, :, :, 0] = 0
    return {"x": x.reshape(N, 128, 4 * C), "u": u.reshape(N, 128, 512), "v": d["v"], **stored(k), **weights(rng, w)}
def setup_inputs_near(rng):
    d = numbers_of(rng)
    o, e = rng.permutation(N) % 2, rng.permutation(N)
    k = np.where(o == 0, 2.0 ** -27, 1.0)
    m = np.where(o == 0, 2.0 ** -30, 1.0)
    s = rng.integers(-1, 2, (N, 8, C))
    s[e[0]] = 0
    s[e[1]] = 1
    x = d["x"].astype(np.float32).reshape(N, 8, 16, C, 4)
    x[o == 0] = 0
    x[:, :, :3] = 0
    x[:, :, 8:] = 0
    x[:, :, 0, :, 0] = np.where(s == 0, 1.0, 1.125 * s) * k[:, None, None]
    x[:, :, 1, :, 0] = np.where(s == 0, -1.125, -1.25 * s) * k[:, None, None]
    x[:, :, 3, :, 0] = k[:, None, None]
    x[:, :, 8, :, 0] = rng.choice([-1.0, 1.0], (N, 8, C)) * 2.0 ** -30
    x[:, :, 9, :, 0] = 2.0 ** -26
    for r in range(N):
        for g in rng.permutation(8)[:4]: x[r, g, 0, rng.integers(C), 0] = 2.0 ** 30 * rng.choice([-1.0, 1.0])
    u = d["u"].reshape(N, 128, 128, 4)
    u[:, :, ::16] = 0
    for h in range(0, 128, 16):
        u[:, h, h, 0] = (1.125 * m).astype(np.float32).astype(BF)
        u[:, h + 1, h, 0] = m.astype(np.float32).astype(BF)
        u[:, h + 2, h, 0] = m.astype(np.float32).astype(BF)
    w = layers(rng)
    w[:, :, :, :, :, :10] = 0
    for g in range(8): w[:, g, 8, 0, g, 2, 0] = 2.0 ** -7
    return {"x": x.reshape(N, 128, 4 * C).astype(BF), "u": u.reshape(N, 128, 512), "v": d["v"], **lists(rng), **weights(rng, w)}
def setup_inputs_odd(rng):
    d = numbers_of(rng)
    e = (PARITY[:, None] + rng.permutation(8)) % 2
    a = 1.0 + (2 * rng.integers(0, 64, (N, 8, 16, C, 4)) + 1) * 2.0 ** -7
    x = np.zeros((N, 8, 16, C, 4))
    x[:, :, :8] = a[:, :, :8] * np.exp2(-rng.integers(0, 7, (N, 8, 8, C, 4)).astype(np.float64)) * rng.choice([-1.0, 1.0], (N, 8, 8, C, 4))
    x[:, :, 0] = 0
    x[:, :, 0, :, 0] = 1.96875 * 2.0 ** 8 * rng.choice([-1.0, 1.0], (N, 8, C))
    x[:, :, 8:] = np.where(e[:, :, None, None, None] == 0, a[:, :, 8:] * np.exp2(12.0 - rng.integers(8, 15, (N, 8, 8, C, 4))), 0.0)
    x[:, :, 8, :, 0] = (np.where(e == 0, -1.0, 1.0) * 1.96875 * 2.0 ** 12)[:, :, None]
    u = d["u"].reshape(N, 128, 128, 4)
    u[:, 8::16, ::16] = 0
    w = layers(rng)
    for i in (0, 8):
        w[:, :, i] = 0
        w[:, :, :, :, :, i] = 0
    for g in rng.permutation(8)[:4]:
        x[:, g, :3] = 0
        x[:, g, 0, :, 0] = 1.96875 * 2.0 ** 8
        x[:, g, 1, :, 0] = (8 + rng.integers(-1, 2, (N, C))) * 2.0 ** -8
        x[:, g, 2, :, 0] = -2.0 ** -5
        x[:, g, 8:] = 0
        x[:, g, 8, :, 0] = 1.96875 * 2.0 ** 12
        x[:, g, 9] = rng.integers(1, 16, (N, C, 4)) * 2.0 ** -4
        u[:, 16 * g, ::16] = 0
        u[:, :, 16 * g] = 0
        u[:, 16 * g + 1:16 * g + 3, 16 * g, 0] = 1
        w[:, :, :, :, g] = 0
        for i in (0, 8): w[:, g, i, 0, g, i, 0] = -0.5
        for b in range(4): w[:, g, 9, b, g, 10, b] = 256.0
    return {"x": x.astype(np.float32).reshape(N, 128, 4 * C).astype(BF), "u": u.reshape(N, 128, 512), "v": d["v"], **lists(rng), **weights(rng, w)}
def setup_inputs_ends(rng):
    d = numbers_of(rng)
    x = np.zeros((N, 8, 16, C, 4))
    u = d["u"].astype(np.float32).reshape(N, 128, 128, 4)
    v = np.zeros((N, 128, 512))
    w = np.zeros((N, 128, 4, 128, 4), np.float32)
    o = rng.permutation(N) % 4
    third, others = np.flatnonzero(o == 2), np.flatnonzero(o != 2)
    if len(third) == 2 and third[0] ^ third[1] == MASK[0]:
        p = rng.choice(others)
        o[third[1]] = o[p]
        o[p] = 2
    i, at = np.arange(128), np.arange(C)
    k = np.zeros((N, 8, C), np.int64)
    for r in range(N):
        h = rng.permutation(8)
        c = np.where(h < 2, 0.0, h % 2 * 2.0 - 1.0)[None, :, None]
        low = -(0.9 + 0.1 * rng.random((8, 16, C, 4))) * 2.0 ** 30
        if o[r] == 0: x[r] = low
        if o[r] == 1: x[r] = low * rng.choice([-1.0, 1.0], C)[:, None]
        if o[r] == 2: x[r] = -(1.0 + 0.125 * rng.integers(0, 8, (8, 16, C, 4))) * 2.0 ** -30
        if o[r] == 3: x[r] = d["x"][r].astype(np.float32).reshape(8, 16, C, 4)[:, :, :1]
        if o[r] < 2:
            u[r, :, ::16] = c * (0.9 + 0.1 * rng.random((128, 8, 4))) * 2.0 ** 30
            v[r] = rng.choice([-1.0, 1.0], (128, 512)) * (0.9 + 0.1 * rng.random((128, 512))) * 2.0 ** 30
        else: v[r] = rng.choice([-1.0, 1.0], (128, 512)) * (1.0 + 0.125 * rng.integers(0, 8, (128, 512))) * 2.0 ** -30
        if o[r] == 2: u[r, :, ::16] = c * (1.0 + 0.125 * rng.integers(0, 8, (128, 8, 4))) * 2.0 ** -30
        if o[r] == 3: u[r, :, ::16] *= np.abs(c).astype(np.float32)
        t = np.array([4.0, 8.0, 16.0])[rng.permutation(8) % 3]
        if o[r] == 2: t[:] = 2.0 ** -8
        if o[r] == 3: t[:] = 2.0 ** 5
        for b in range(4): w[r, i, b, i, b] = t[i // 16]
        for g, n in enumerate(rng.permutation(8) % 5): k[r, g] = [at, at[::-1], np.roll(at, -1), at ^ 1, rng.permutation(C)][n]
    return {"x": x.astype(np.float32).reshape(N, 128, 4 * C).astype(BF), "u": u.reshape(N, 128, 512).astype(BF), "v": v.astype(np.float32).astype(BF), **stored(k), **weights(rng, w.astype(BF))}
def setup_inputs_spread(rng):
    d = numbers_of(rng)
    w = layers(rng).reshape(N, 128, 4, 128, 4)
    i, r = np.arange(128), int(rng.integers(N))
    for b in range(4): w[r, i, b, i, b] = 256.0
    return {"x": wide(rng, N, 128, 4 * C, cols=6), "u": d["u"], "v": d["v"], **lists(rng), **weights(rng, w)}
def check_inputs(d):
    b = []
    for k in ("x", "u", "v"):
        a = np.abs(d[k].astype(np.float32))
        if not (np.isfinite(a).all() and ((a == 0) | (a >= 2.0 ** -30) & (a <= 2.0 ** 30)).all()): b.append("a value of " + k)
    none, least, most = [emit(mx_ref.quantize(np.full((128, 16), k, np.float32).astype(BF)))[1][0, 0] for k in (0.0, 2.0 ** -8, 2.0 ** 8)]
    for r in range(N):
        if not (np.sort(gentries(d["fl"][r]), axis=1) == np.arange(C)).all(): b.append("fl: a group's entries are no permutation")
        if ((d["wc"][r] == 0x7F) | (d["wc"][r] == 0xFF)).any(): b.append("wc: a code that is no number")
        s = mx_ref.live(d["ws"][r])
        if ((s != none) & ((s < least) | (s > most))).any(): b.append("ws: a scale out of range")
        if (((d["wc"][r].reshape(16, 8, 512, 4) & 0x7F) != 0) & (s == none)[:, None, :, None]).any(): b.append("wc: a code other than zero under the scale of zeros")
    return b
def returns(e, gate):
    at = np.tile(np.arange(C), (8, 1))
    step = np.where(gate, at, e)
    a = e
    for i in range(C): a = np.take_along_axis(step, a, axis=1)
    return np.where(gate, a, at)
def reference(x, u, v, fl, wc, ws):
    half = np.float32(0.5)
    qu = [mx_ref.quantize(u[r]) for r in range(N)]
    lay = [pk(wc[r], ws[r]) for r in range(N)]
    own = [gentries(fl[r]).astype(np.int64) for r in range(N)]
    now = [x[r] for r in range(N)]
    for m in MASK:
        q = [mx_ref.quantize(now[r]) for r in range(N)]
        t = [decode(q[r]) for r in range(N)]
        bit = [mx_ref.matmul(qu[r], q[r])[::16] > 0 for r in range(N)]
        made, new = [], []
        for r in range(N):
            d = r ^ m
            a = returns(own[d], bit[r] != bit[d])
            n = np.take_along_axis(own[r], a, axis=1)
            z = (gcols(t[r].astype(BF), n).astype(np.float32) + gcols(t[d].astype(BF), a).astype(np.float32)) * half
            qz = mx_ref.quantize(z.astype(BF))
            back = np.argsort(n, axis=1)
            p = [mx_ref.matmul(pick(lay[r], np.arange(128 * b, 128 * b + 128)), qz) * np.float32(0.03125) for b in range(4)]
            made.append(tile([(t[r][:, b::4] + gpick(p[b], back)) * half for b in range(4)]))
            new.append(n)
        now, own = made, new
    y, ln = np.zeros((N, 128, C), np.float32), np.zeros((N, 8, C), np.float32)
    oc, osc = np.zeros((N, 128, 4 * C), np.uint8), np.zeros((N, 16, C), np.uint8)
    for r in range(N):
        q = mx_ref.quantize(now[r])
        y[r] = mx_ref.matmul(mx_ref.quantize(v[r]), q)
        ln[r] = own[r]
        oc[r], osc[r] = emit(q)
    return {"y": y, "ln": ln, "oc": oc, "osc": osc}

@@ -1,0 +1,308 @@
+from concourse.mybir import dt, AluOpType as OP, ActivationFunctionType as ACT
+
+C = 384
+K = C // 16
+H = 192
+B = 256
+MASKS = (1, 2, 3)
+MID = 192
+BIG = 2.0 ** 22
+
+SCRATCH = {}
+def _buffers(where, kind, **widths):
+    for name, width in widths.items(): SCRATCH[name] = (where, [128, width], kind)
+_buffers("sbuf", "bfloat16", wi=2 * C, m16=16, msk=C, eb0=520, eb=520, ut=512, vt=512, xt=4 * C, xp=4 * C, zt=4 * C, fh=4 * C,
+         brow=C, bsc=C, fc=K, msg=6 * K, row=2 * C, scan=C, arow=C, ainv=C, ginv=C, isc=C, frow=2 * C, rsc=C, le0=K, lb0=K, lb1=2 * K, lb2=2 * K)
+_buffers("sbuf", "int32", dmod=16, dmod2=16, pt=K, pt2=K, st=K, ui=8, fl32=K)
+_buffers("sbuf", "float32", m1=16, m2=16, cc=K, scc=4, gs=4 * C, pc=4 * C, p3=C, gate=K, dif=K, w1=K, w2=K, w3=K, w4=K, lnf=C, ysb=C)
+_buffers("sbuf", "uint16", poff=K, uoff=8, tab=2 * K, fin=K, atab=K, inv=2 * K, ftab=K, f4=4 * K)
+_buffers("sbuf", "float8_e4m3fn_x4", ebq=512, uq=128, urq=128, vq=128, wq=512, qx=4 * C, qp=C, qz=C, lc0=C, lc1=C, lc2=C)
+_buffers("sbuf", "uint8", ebs=512, us=128, urs=128, vs=128, wss=512, sx=4 * C, sp=C, sz=C, lp0=C, lp1=C, lp2=C)
+_buffers("psum", "float32", ps0=512, ps1=512, ps2=512, ps3=512, ps4=512, ps5=512, ps6=512, ps7=512)
+
+SEMAPHORES = ["cv", "cs", "ct", "cg", "sent", "ae0"]
+SEMAPHORES += ["%s%d" % (_k, _n) for _k in ("ab", "ac", "ap") for _n in range(3)]
+SEMAPHORES += ["dx", "dx2", "du", "dv", "df", "dw", "dws", "oy0", "oy1", "ol", "oc", "os0", "os1", "os2", "os3"]
+
+OWN_SLOTS = {1: 1, 2: 1, 3: 1, 4: 1}
+SUM_SLOTS = {6: 2, 7: 3}
+
+
+def rank_program(g, core, T, topo):
+    rank = T.rank_of(core)
+    if rank is None:
+        return
+    queue = {"v": g.vector, "s": g.scalar, "t": g.tensor, "g": g, "y": g.sync}
+    counter = {"v": "cv", "s": "cs", "t": "ct", "g": "cg"}
+    total = {}
+    known = {q: {} for q in queue}
+    clock = {}
+    book = {}
+
+    def wait(q, tok):
+        k = known[q]
+        if k.get(tok[0], 0) < tok[1]:
+            queue[q].wait_ge(T.sem[tok[0]], tok[1])
+            for s, v in list(clock.get(tok, {}).items()) + [tok]:
+                if k.get(s, 0) < v: k[s] = v
+
+    def meets(x, y):
+        if max(x[0], y[0]) >= min(x[1], y[1]): return False
+        return not (x[2] == y[2] > 1 and (x[0] - y[0]) % x[2])
+
+    def covers(x, y):
+        return x[0] <= y[0] and y[1] <= x[1] and (x[2] == 1 or (x[2] == y[2] and (x[0] - y[0]) % x[2] == 0))
+
+    def span(v):
+        return (0, 512, 1) if v[0][:2] == "ps" else v[1:]
+
+    def need(q, rd, wr, joins=False):
+        toks = {}
+        for v in rd + wr:
+            w = v in wr or v[0][:2] == "ps"
+            for isw, s, tok in book.get(v[0], []):
+                if (w or isw) and meets(span(v), s) and not (joins and v in wr and tok[0] == counter[q]):
+                    toks[tok[0]] = max(toks.get(tok[0], 0), tok[1])
+        for s in sorted(toks, key=lambda s: s in ("cv", "cs", "ct", "cg")):
+            wait(q, (s, toks[s]))
+
+    def note(rd, wr, tok):
+        for v in wr + rd:
+            w = v in wr or v[0][:2] == "ps"
+            b = book.setdefault(v[0], [])
+            if w: b[:] = [r for r in b if not covers(span(v), r[1])]
+            b.append((w, span(v), tok))
+
+    def do(q, call, rd, wr, joins=False, sem=None, n=1):
+        need(q, rd, wr, joins)
+        s = sem or counter[q]
+        total[s] = total.get(s, 0) + n
+        tok = (s, total[s])
+        call().then_inc(T.sem[s], n)
+        clock[tok] = dict(known[q])
+        note(rd, wr, tok)
+
+    def V(name, a=0, b=None, step=1):
+        return (name, a, SCRATCH[name][1][1] if b is None else b, step)
+
+    def ap(v):
+        n, a, b, st = v
+        return T[n][:, a:b] if st == 1 else T[n][:, a:b:st]
+
+    def load(q, out, src, sem, codes=False):
+        dst = ap(out).bitcast(dt.uint8) if codes else ap(out)
+        do(q, lambda: queue[q].dma_start(dst, src), [], [out], sem=sem, n=16)
+
+    def copy(out, in_):
+        do("v", lambda: g.vector.tensor_copy(ap(out), ap(in_)), [in_], [out])
+
+    def act(out, in_, scale=1.0, func=ACT.Copy):
+        do("s", lambda: g.scalar.activation(ap(out), ap(in_), func, scale=scale), [in_], [out])
+
+    def ts(out, in_, s1, op0, s2=None, op1=None, extra=()):
+        if op1 is None: do("v", lambda: g.vector.tensor_scalar(ap(out), ap(in_), s1, None, op0), [in_] + list(extra), [out])
+        else: do("v", lambda: g.vector.tensor_scalar(ap(out), ap(in_), s1, s2, op0, op1), [in_] + list(extra), [out])
+
+    def tt(out, a, b, op):
+        do("v", lambda: g.vector.tensor_tensor(ap(out), ap(a), ap(b), op), [a, b], [out])
+
+    def pick(q, out, win, off):
+        if q == "v": do("v", lambda: g.vector.tensor_copy(ap(out), ap(win).indirect(ap(off))), [win, off], [out])
+        else: do("s", lambda: g.scalar.activation(ap(out), ap(win).indirect(ap(off)), ACT.Copy), [win, off], [out])
+
+    def pickadd(out, win, off, other):
+        do("v", lambda: g.vector.tensor_tensor(ap(out), ap(win).indirect(ap(off)), ap(other), OP.add), [win, off, other], [out])
+
+    def lay(win, off, in_):
+        do("v", lambda: g.vector.tensor_copy(ap(win).indirect(ap(off)), ap(in_)), [in_, off], [win])
+
+    def quant(q, s, t):
+        do("v", lambda: g.vector.quantize_mx(ap(q), ap(s), ap(t)), [t], [q, s])
+
+    def quant2(q, s, at, t):
+        for a, b in ((0, B), (B, C)): quant(V(q, at + a, at + b), V(s, at + a, at + b), V(t, 4 * a, 4 * b))
+
+    def mm(bank, a, b, wq, ws, xq, xs, start=True, stop=True):
+        out = V("ps%d" % bank, a, b)
+        do("t", lambda: g.tensor.matmul_mx(ap(out), ap(wq), ap(ws), ap(xq), ap(xs), start, stop), [wq, ws, xq, xs], [out], joins=not start)
+
+    def diag(sc, row):
+        do("v", lambda: g.vector.tensor_tensor_scan(ap(sc), ap(V("msk")), ap(row), 0.0, OP.mult, OP.add), [V("msk"), row], [sc])
+
+    def table(out, sc, mul=0, add=MID + 0.25):
+        ts(out, V(sc[0], 15, C, 16), T.scc[:, mul:mul + 1], OP.mult, add, OP.add, extra=[V("scc")])
+
+    def pick2(out, win, off):
+        pick("s", V(out[0], out[1] + H, out[2]), win, V(off[0], off[1] + H // 16, off[2]))
+        pick("v", V(out[0], out[1], out[1] + H), win, V(off[0], off[1], off[1] + H // 16))
+
+    def send(dst, out, in_, sem, codes=False):
+        need("g", [in_], [])
+        rid, pid, _e = topo.addr(dst)
+        o, i = (ap(out).bitcast(dt.uint8), ap(in_).bitcast(dt.uint8)) if codes else (ap(out), ap(in_))
+        g.remote_dma(o, i, T.sem[sem], T.sem["sent"], pid, rid, topo.mask(core, dst))
+        total["sent"] = total.get("sent", 0) + len(topo.engines(core, dst))
+
+    def arrives(name, sem, src):
+        tok = (sem, len(topo.engines(src, core)))
+        total[sem] = tok[1]
+        note([], [V(name)], tok)
+
+    partner = [T.cores[rank ^ m] for m in MASKS]
+    iota_win = V("wi", C, 2 * C)
+    arrives("le0", "ae0", partner[0])
+    for n in range(3):
+        for k, s in (("lb", "ab"), ("lc", "ac"), ("lp", "ap")):
+            arrives("%s%d" % (k, n), "%s%d" % (s, n), partner[n])
+
+    load("y", V("fl32"), T.fl[:, :], "df")
+    load("y", V("xt", 0, 4 * B), T.x[:, 0:4 * B], "dx")
+    load("s", V("ut"), T.u[:, :], "du")
+    load("s", V("xt", 4 * B, 4 * C), T.x[:, 4 * B:4 * C], "dx2")
+    wait("y", ("dx", 16))
+    wait("y", ("dx2", 16))
+    load("y", V("wq"), T.wc[:, :], "dw", codes=True)
+    load("y", V("wss"), T.ws[:, :], "dws")
+    load("y", V("vt"), T.v[:, :], "dv")
+
+    def iota(out, pattern, base, cm):
+        do("g", lambda: g.iota(ap(out), pattern, base, cm, allow_small_or_imprecise_dtypes=True), [], [out])
+    do("v", lambda: g.vector.memset(T.eb0[:, :], 0.5), [], [V("eb0")])
+    iota(V("dmod"), [[1, 16]], 0, -1)
+    iota(V("pt"), [[0, K]], 0, 1)
+    iota(V("ui"), [[16, 8]], 0, 0)
+    iota(V("st"), [[16, K]], -MID, 0)
+    do("g", lambda: g.affine_select(T.eb[:, :], T.eb0[:, :], [[1, 520]], OP.is_equal, 0.0, -4, -4), [V("eb0")], [V("eb")])
+    iota(iota_win, [[1, C]], -MID, 0)
+    ts(V("dmod2"), V("dmod"), 15, OP.bitwise_and)
+    ts(V("m1"), V("dmod2"), 1.0, OP.is_equal, BIG - 1.0, OP.mult)
+    ts(V("m2"), V("dmod2"), 0.0, OP.not_equal)
+    tt(V("m16"), V("m1"), V("m2"), OP.add)
+    ts(V("pt2"), V("pt"), 15, OP.bitwise_and)
+    copy(V("poff"), V("pt2"))
+    pick("s", V("msk"), V("m16"), V("poff"))
+    copy(V("uoff"), V("ui"))
+    tt(V("cc"), V("pt2"), V("st"), OP.add)
+    ts(V("scc", 0, 1), V("pt2", 0, 1), 15.0, OP.is_equal, 1.0 - 1.0 / BIG, OP.mult)
+    ts(V("scc", 0, 1), V("scc", 0, 1), 1.0 / BIG, OP.add)
+    ts(V("scc", 1, 2), V("scc", 0, 1), 4.0, OP.mult)
+    for b in range(4): quant(V("ebq", 128 * b, 128 * b + 128), V("ebs", 128 * b, 128 * b + 128), V("eb", 4 - b, 516 - b))
+
+    ts(V("fc"), V("fl32"), -float(MID), OP.add)
+    send(partner[0], V("le0"), V("fc"), "ae0")
+    copy(V("ftab"), V("fl32"))
+    for b in range(4):
+        ts(V("f4", K * b, K * b + K), V("fl32"), 4.0, OP.mult, float(b), OP.add)
+    quant(V("uq"), V("us"), V("ut"))
+    do("v", lambda: g.vector.tensor_copy(T.urq[:, :].bitcast(dt.uint32), T.uq[:, :].bitcast(dt.uint32).indirect(T.uoff[:, 0:8])), [V("uq"), V("uoff")], [V("urq")])
+    pick("s", V("urs"), V("us"), V("uoff"))
+    pick("s", V("frow", 0, C), iota_win, V("ftab"))
+
+    def col(name, n): return V(name, C * n, C * n + C)
+    def E(b): return V("ebq", 128 * b, 128 * b + 128), V("ebs", 128 * b, 128 * b + 128)
+    def W(b): return V("wq", 128 * b, 128 * b + 128), V("wss", 128 * b, 128 * b + 128)
+    def bit_of(name, b): return V(name, b, 4 * C, 4)
+
+    for n in range(3):
+        qx, sx = col("qx", n), col("sx", n)
+        cur, nxt = n % 2, (n + 1) % 2
+        frow, invf = col("frow", cur), V("inv", K * cur, K * cur + K)
+        mlist, bt = V("msg", 2 * K * n, 2 * K * n + K), V("msg", 2 * K * n + K, 2 * K * n + 2 * K)
+        quant2("qx", "sx", C * n, "xt")
+        mm(0, 0, B, V("urq"), V("urs"), V("qx", C * n, C * n + B), V("sx", C * n, C * n + B))
+        mm(1, 0, C - B, V("urq"), V("urs"), V("qx", C * n + B, C * n + C), V("sx", C * n + B, C * n + C))
+        act(V("brow", B, C), V("ps1", 0, C - B), func=ACT.Sign)
+        ts(V("brow", 0, B), V("ps0", 0, B), 0.0, OP.is_gt)
+        if n: diag(V("rsc"), frow)
+        diag(V("bsc"), V("brow"))
+        if n: ts(mlist, V("rsc", 15, C, 16), T.scc[:, 0:1], OP.mult, extra=[V("scc")])
+        ts(bt, V("bsc", 15, C, 16), T.scc[:, 0:1], OP.mult, 0.5, OP.is_gt, extra=[V("scc")])
+        if n: send(partner[n], V("lb%d" % n), V("msg", 2 * K * n, 2 * K * n + 2 * K), "ab%d" % n)
+        else: send(partner[n], V("lb0"), bt, "ab0")
+        send(partner[n], V("lc%d" % n), qx, "ac%d" % n, codes=True)
+        send(partner[n], V("lp%d" % n), sx, "ap%d" % n)
+        if n:
+            for b in range(4): table(V("f4", K * b, K * b + K), V("rsc"), 1, 4.0 * MID + b + 0.25)
+        for b in range(4): mm(4 + b, 0, C, *E(b), qx, sx)
+        for b in (0, 1): pick("s", bit_of("xp", b), V("xt"), V("f4", K * b, K * b + K))
+        for b in (2, 3): pick("v", bit_of("xp", b), V("xt"), V("f4", K * b, K * b + K))
+        quant(V("qp"), V("sp"), V("xp"))
+        def halves(out, bank):
+            todo = [(b, h) for b in range(4) for h in range(2)]
+            def some(k):
+                for b, h in todo[:k]: act(V(out, C * b + H * h, C * b + H * h + H), V("ps%d" % (bank + b), H * h, H * h + H))
+                del todo[:k]
+            return some
+        numbers, sums = halves("fh", 4), halves("gs", 0)
+        numbers(4)
+        for b in range(4): mm(b, 0, C, *E(b), V("qp"), V("sp"), True, False)
+        if n == 0:
+            lay(V("ainv"), V("ftab"), iota_win)
+            diag(V("isc"), V("ainv"))
+            table(invf, V("isc"))
+        le = V("lb%d" % n, 0, K) if n else V("le0")
+        lb = V("lb%d" % n, K, 2 * K) if n else V("lb0")
+        tt(V("dif"), V("cc"), le, OP.subtract)
+        tt(V("gate"), bt, lb, OP.not_equal)
+        tt(V("w1"), V("gate"), V("dif"), OP.mult)
+        tt(V("w2"), V("w1"), le, OP.add)
+        tab = [V("tab", K * i, K * i + K) for i in range(2)]
+        row = [col("row", i) for i in range(2)]
+        ts(tab[0], V("w2"), MID + 0.25, OP.add)
+        for b in range(4): mm(b, 0, C, *E(b), V("lc%d" % n), V("lp%d" % n), False, True)
+        spare = [lambda: ts(V("w3"), V("gate"), -float(C), OP.mult, C + MID + 0.25, OP.add), lambda: tt(V("w4"), V("cc"), V("w1"), OP.subtract),
+                 lambda: tt(V("w4"), V("w3"), V("w4"), OP.add), lambda: copy(V("fin"), V("w4"))]
+        pick2(row[0], iota_win, tab[0])
+        for lv in range(1, 8):
+            o, w = (lv - 1) % 2, lv % 2
+            pick2(row[w], row[o], tab[o])
+            numbers(OWN_SLOTS.get(lv, 0))
+            sums(SUM_SLOTS.get(lv, 0))
+            diag(V("scan"), row[w])
+            if spare: spare.pop(0)()
+            table(tab[w], V("scan"))
+        pick2(row[0], row[1], tab[1])
+        pick2(V("wi", 0, C), row[0], tab[1])
+        pick2(V("arow"), V("wi"), V("fin"))
+        sums(8)
+        diag(V("scan"), V("arow"))
+        at = V("atab")
+        table(at, V("scan"))
+        for b in range(3): pick("s", bit_of("zt", b), col("gs", b), at)
+        lay(V("ainv"), at, iota_win)
+        pick("v", bit_of("zt", 3), col("gs", 3), at)
+        quant2("qz", "sz", 0, "zt")
+        mm(4, 0, B, *W(0), V("qz", 0, B), V("sz", 0, B))
+        mm(0, 0, C - B, *W(0), V("qz", B, C), V("sz", B, C))
+        for b in range(1, 4): mm(4 + b, 0, C, *W(b), V("qz"), V("sz"))
+        mm(3, 0, C, *E(3), qx, sx)
+        if n == 1: quant(V("vq"), V("vs"), V("vt"))
+        pick("s", V("ginv"), V("ainv"), invf)
+        diag(V("isc"), V("ginv"))
+        ts(V("pc", 0, B), V("ps4", 0, B), 2.0 ** -6, OP.mult)
+        invr = V("inv", K * nxt, K * nxt + K)
+        table(invr, V("isc"))
+        act(V("pc", B, C), V("ps0", 0, C - B), scale=2.0 ** -6)
+        for b in range(1, 4): act(col("pc", b), V("ps%d" % (4 + b), 0, C), scale=2.0 ** -6)
+        pick("s", V("p3"), col("pc", 3), invr)
+        pick("s", col("frow", nxt), frow, at)
+        for b in range(3): pickadd(bit_of("xt", b), col("pc", b), invr, col("fh", b))
+        tt(bit_of("xt", 3), V("ps3", 0, C), V("p3"), OP.add)
+
+    def store(q, dst, in_, sem, codes=False, a=None):
+        src = a if a is not None else (ap(in_).bitcast(dt.uint8) if codes else ap(in_))
+        do(q, lambda: queue[q].dma_start(dst, src), [in_], [], sem=sem, n=16)
+    quant2("qx", "sx", 3 * C, "xt")
+    do("s", lambda: g.scalar.activation(T.lnf[:, :], ap(col("frow", 1)), ACT.Identity, bias=float(MID)), [col("frow", 1)], [V("lnf")])
+    store("y", T.oc[:, :], col("qx", 3), "oc", codes=True)
+    for b in range(2):
+        mm(b, 0, H, V("vq"), V("vs"), V("qx", 3 * C + H * b, 3 * C + H * b + H), V("sx", 3 * C + H * b, 3 * C + H * b + H))
+    for k in range(4):
+        store("y" if k < 2 else "s", T.osc[4 * k:4 * k + 4, :], col("sx", 3), "os%d" % k, a=T.sx[32 * k:32 * k + 4, 3 * C:4 * C])
+    copy(V("ysb", 0, H), V("ps0", 0, H))
+    act(V("ysb", H, C), V("ps1", 0, H))
+    store("y", T.y[:, 0:H], V("ysb", 0, H), "oy0")
+    store("s", T.y[:, H:C], V("ysb", H, C), "oy1")
+    store("y", T.ln[:, :], V("lnf"), "ol", a=T.lnf[0:128:16, :])
+    for s in sorted(total):
+        wait("g", (s, total[s]))

@@ -12,20 +12,24 @@ SCRATCH = {}
 def _buffers(where, kind, **widths):
     for name, width in widths.items(): SCRATCH[name] = (where, [128, width], kind)
 _buffers("sbuf", "bfloat16", wi=2 * C, m16=16, msk=C, eb0=520, eb=520, ut=512, vt=512, xt=4 * C, xp=4 * C, zt=4 * C, fh=4 * C,
-         brow=C, bsc=C, fc=K, msg=6 * K, row=2 * C, scan=C, arow=C, ainv=C, ginv=C, isc=C, frow=2 * C, rsc=C, le0=K, lb0=K, lb1=2 * K, lb2=2 * K)
-_buffers("sbuf", "int32", dmod=16, dmod2=16, pt=K, pt2=K, st=K, ui=8, fl32=K)
-_buffers("sbuf", "float32", m1=16, m2=16, cc=K, scc=4, gs=4 * C, pc=4 * C, p3=C, gate=K, dif=K, w1=K, w2=K, w3=K, w4=K, lnf=C, ysb=C)
+         brow=C, bsc=C, msg=6 * K, row=2 * C, scan=C, arow=C, ainv=C, ginv=C, isc=C, frow=2 * C, rsc=C, mq=2 * K, lb0=2 * K, lb1=2 * K, lb2=2 * K)
+_buffers("sbuf", "int32", dmod=16, dmod2=16, pt=K, pt2=K, st=K, ui=8, fl32=3 * K, le0=K, le1=K, le2=K)
+_buffers("sbuf", "float32", m1=16, m2=16, cc=K, scc=4, gs=4 * C, pc=4 * C, p3=C, w0=2 * K, w1=2 * K, w2=2 * K, w3=K, t1=2 * K, t2=2 * K, lnf=C, ysb=C)
 _buffers("sbuf", "uint16", poff=K, uoff=8, tab=2 * K, fin=K, atab=K, inv=2 * K, ftab=K, f4=4 * K)
 _buffers("sbuf", "float8_e4m3fn_x4", ebq=512, uq=128, urq=128, vq=128, wq=512, qx=4 * C, qp=C, qz=C, lc0=C, lc1=C, lc2=C)
 _buffers("sbuf", "uint8", ebs=512, us=128, urs=128, vs=128, wss=512, sx=4 * C, sp=C, sz=C, lp0=C, lp1=C, lp2=C)
 _buffers("psum", "float32", ps0=512, ps1=512, ps2=512, ps3=512, ps4=512, ps5=512, ps6=512, ps7=512)
 
-SEMAPHORES = ["cv", "cs", "ct", "cg", "sent", "ae0"]
-SEMAPHORES += ["%s%d" % (_k, _n) for _k in ("ab", "ac", "ap") for _n in range(3)]
-SEMAPHORES += ["dx", "dx2", "du", "dv", "df", "dw", "dws", "oy0", "oy1", "ol", "oc", "os0", "os1", "os2", "os3"]
+SEMAPHORES = ["cv", "cs", "ct", "cg", "sent"]
+SEMAPHORES += ["%s%d" % (_k, _n) for _k in ("ae", "ab", "ac", "ap") for _n in range(3)]
+SEMAPHORES += ["dx", "dx2", "du", "dv", "df", "dw", "dws", "oy0", "oy1", "ol", "oc0", "oc1", "os0", "os1", "os2", "os3"]
 
-OWN_SLOTS = {1: 1, 2: 1, 3: 1, 4: 1}
-SUM_SLOTS = {6: 2, 7: 3}
+STEPS = ["P", "T", "P", "T", "P", "T", "P", "T", "P", "T", "P", "T2", "P", "T3", "P", "P"]
+HELP = 96
+OWN_V = 0
+XP_S = 3
+OWN_T = 6
+TAIL = 1
 
 
 def rank_program(g, core, T, topo):
@@ -61,7 +65,9 @@ def rank_program(g, core, T, topo):
         for v in rd + wr:
             w = v in wr or v[0][:2] == "ps"
             for isw, s, tok in book.get(v[0], []):
-                if (w or isw) and meets(span(v), s) and not (joins and v in wr and tok[0] == counter[q]):
+                own = tok[0] == counter.get(q)
+                if own and v[0][:2] == "ps" and v not in wr: continue
+                if (w or isw) and meets(span(v), s) and not (joins and v in wr and own):
                     toks[tok[0]] = max(toks.get(tok[0], 0), tok[1])
         for s in sorted(toks, key=lambda s: s in ("cv", "cs", "ct", "cg")):
             wait(q, (s, toks[s]))
@@ -89,9 +95,19 @@ def rank_program(g, core, T, topo):
         n, a, b, st = v
         return T[n][:, a:b] if st == 1 else T[n][:, a:b:st]
 
+    def part(v, a, b):
+        return (v[0], v[1] + a * v[3], min(v[2], v[1] + b * v[3]), v[3])
+
     def load(q, out, src, sem, codes=False):
         dst = ap(out).bitcast(dt.uint8) if codes else ap(out)
         do(q, lambda: queue[q].dma_start(dst, src), [], [out], sem=sem, n=16)
+
+    def store(q, dst, in_, sem, codes=False, a=None):
+        src = a if a is not None else (ap(in_).bitcast(dt.uint8) if codes else ap(in_))
+        do(q, lambda: queue[q].dma_start(dst, src), [in_], [], sem=sem, n=16)
+
+    def fill(out, value):
+        do("v", lambda: g.vector.memset(ap(out), value), [], [out])
 
     def copy(out, in_):
         do("v", lambda: g.vector.tensor_copy(ap(out), ap(in_)), [in_], [out])
@@ -106,11 +122,16 @@ def rank_program(g, core, T, topo):
     def tt(out, a, b, op):
         do("v", lambda: g.vector.tensor_tensor(ap(out), ap(a), ap(b), op), [a, b], [out])
 
-    def pick(q, out, win, off):
+    def scan(out, d0, d1, first=0.0, op0=OP.mult):
+        do("v", lambda: g.vector.tensor_tensor_scan(ap(out), ap(d0), ap(d1), first, op0, OP.add), [d0, d1], [out])
+
+    def pick(q, out, win, off, a=0, b=C):
+        out, off = part(out, a, b), part(off, a // 16, b // 16)
         if q == "v": do("v", lambda: g.vector.tensor_copy(ap(out), ap(win).indirect(ap(off))), [win, off], [out])
         else: do("s", lambda: g.scalar.activation(ap(out), ap(win).indirect(ap(off)), ACT.Copy), [win, off], [out])
 
-    def pickadd(out, win, off, other):
+    def pickadd(out, win, off, other, a=0, b=C):
+        out, off, other = part(out, a, b), part(off, a // 16, b // 16), part(other, a, b)
         do("v", lambda: g.vector.tensor_tensor(ap(out), ap(win).indirect(ap(off)), ap(other), OP.add), [win, off, other], [out])
 
     def lay(win, off, in_):
@@ -119,22 +140,22 @@ def rank_program(g, core, T, topo):
     def quant(q, s, t):
         do("v", lambda: g.vector.quantize_mx(ap(q), ap(s), ap(t)), [t], [q, s])
 
-    def quant2(q, s, at, t):
-        for a, b in ((0, B), (B, C)): quant(V(q, at + a, at + b), V(s, at + a, at + b), V(t, 4 * a, 4 * b))
+    def quant2(q, s, at, t, pieces=((0, B), (B, C))):
+        for a, b in pieces: quant(V(q, at + a, at + b), V(s, at + a, at + b), V(t, 4 * a, 4 * b))
 
     def mm(bank, a, b, wq, ws, xq, xs, start=True, stop=True):
         out = V("ps%d" % bank, a, b)
         do("t", lambda: g.tensor.matmul_mx(ap(out), ap(wq), ap(ws), ap(xq), ap(xs), start, stop), [wq, ws, xq, xs], [out], joins=not start)
 
     def diag(sc, row):
-        do("v", lambda: g.vector.tensor_tensor_scan(ap(sc), ap(V("msk")), ap(row), 0.0, OP.mult, OP.add), [V("msk"), row], [sc])
+        scan(sc, V("msk"), row)
 
     def table(out, sc, mul=0, add=MID + 0.25):
         ts(out, V(sc[0], 15, C, 16), T.scc[:, mul:mul + 1], OP.mult, add, OP.add, extra=[V("scc")])
 
     def pick2(out, win, off):
-        pick("s", V(out[0], out[1] + H, out[2]), win, V(off[0], off[1] + H // 16, off[2]))
-        pick("v", V(out[0], out[1], out[1] + H), win, V(off[0], off[1], off[1] + H // 16))
+        pick("s", out, win, off, H, C)
+        pick("v", out, win, off, 0, H)
 
     def send(dst, out, in_, sem, codes=False):
         need("g", [in_], [])
@@ -148,123 +169,139 @@ def rank_program(g, core, T, topo):
         total[sem] = tok[1]
         note([], [V(name)], tok)
 
+    def col(name, n, width=C): return V(name, width * n, width * n + width)
+    def E(b): return col("ebq", b, 128), col("ebs", b, 128)
+    def W(b): return col("wq", b, 128), col("wss", b, 128)
+    def bit_of(name, b): return V(name, b, 4 * C, 4)
+    def even(name): return V(name, 0, 2 * K, 2)
+    def odd(name): return V(name, 1, 2 * K, 2)
+    def some(calls, k=99):
+        for call in calls[:k]: call()
+        del calls[:k]
+
     partner = [T.cores[rank ^ m] for m in MASKS]
     iota_win = V("wi", C, 2 * C)
-    arrives("le0", "ae0", partner[0])
     for n in range(3):
-        for k, s in (("lb", "ab"), ("lc", "ac"), ("lp", "ap")):
+        for k, s in (("le", "ae"), ("lb", "ab"), ("lc", "ac"), ("lp", "ap")):
             arrives("%s%d" % (k, n), "%s%d" % (s, n), partner[n])
 
-    load("y", V("fl32"), T.fl[:, :], "df")
+    load("s", col("fl32", 0, K), T.fl[:, :], "df")
+    load("y", V("ut"), T.u[:, :], "du")
     load("y", V("xt", 0, 4 * B), T.x[:, 0:4 * B], "dx")
-    load("s", V("ut"), T.u[:, :], "du")
-    load("s", V("xt", 4 * B, 4 * C), T.x[:, 4 * B:4 * C], "dx2")
-    wait("y", ("dx", 16))
-    wait("y", ("dx2", 16))
+    load("y", V("xt", 4 * B, 4 * C), T.x[:, 4 * B:4 * C], "dx2")
+    need("y", [V("lp0")], [])
     load("y", V("wq"), T.wc[:, :], "dw", codes=True)
     load("y", V("wss"), T.ws[:, :], "dws")
     load("y", V("vt"), T.v[:, :], "dv")
 
     def iota(out, pattern, base, cm):
         do("g", lambda: g.iota(ap(out), pattern, base, cm, allow_small_or_imprecise_dtypes=True), [], [out])
-    do("v", lambda: g.vector.memset(T.eb0[:, :], 0.5), [], [V("eb0")])
+    fill(V("eb0"), 0.5)
     iota(V("dmod"), [[1, 16]], 0, -1)
     iota(V("pt"), [[0, K]], 0, 1)
     iota(V("ui"), [[16, 8]], 0, 0)
-    iota(V("st"), [[16, K]], -MID, 0)
+    iota(V("st"), [[16, K]], 0, 0)
     do("g", lambda: g.affine_select(T.eb[:, :], T.eb0[:, :], [[1, 520]], OP.is_equal, 0.0, -4, -4), [V("eb0")], [V("eb")])
-    iota(iota_win, [[1, C]], -MID, 0)
+    send(partner[0], V("le0"), col("fl32", 0, K), "ae0")
+    fill(V("msg"), 0.0)
+    scan(iota_win, V("eb0", 0, C), V("eb0", 0, C), -MID - 1.0, OP.add)
     ts(V("dmod2"), V("dmod"), 15, OP.bitwise_and)
+    ts(V("pt2"), V("pt"), 15, OP.bitwise_and)
     ts(V("m1"), V("dmod2"), 1.0, OP.is_equal, BIG - 1.0, OP.mult)
     ts(V("m2"), V("dmod2"), 0.0, OP.not_equal)
-    tt(V("m16"), V("m1"), V("m2"), OP.add)
-    ts(V("pt2"), V("pt"), 15, OP.bitwise_and)
     copy(V("poff"), V("pt2"))
-    pick("s", V("msk"), V("m16"), V("poff"))
     copy(V("uoff"), V("ui"))
+    tt(V("m16"), V("m1"), V("m2"), OP.add)
     tt(V("cc"), V("pt2"), V("st"), OP.add)
-    ts(V("scc", 0, 1), V("pt2", 0, 1), 15.0, OP.is_equal, 1.0 - 1.0 / BIG, OP.mult)
-    ts(V("scc", 0, 1), V("scc", 0, 1), 1.0 / BIG, OP.add)
-    ts(V("scc", 1, 2), V("scc", 0, 1), 4.0, OP.mult)
-    for b in range(4): quant(V("ebq", 128 * b, 128 * b + 128), V("ebs", 128 * b, 128 * b + 128), V("eb", 4 - b, 516 - b))
-
-    ts(V("fc"), V("fl32"), -float(MID), OP.add)
-    send(partner[0], V("le0"), V("fc"), "ae0")
-    copy(V("ftab"), V("fl32"))
-    for b in range(4):
-        ts(V("f4", K * b, K * b + K), V("fl32"), 4.0, OP.mult, float(b), OP.add)
+    ts(V("scc", 3, 4), V("pt2", 0, 1), 15.0, OP.is_equal)
+    pick("s", V("msk"), V("m16"), V("poff"))
+    fill(even("mq"), 0.0)
+    fill(odd("mq"), 0.25)
+    ts(V("scc", 0, 1), V("scc", 3, 4), 1.0 - 1.0 / BIG, OP.mult, 1.0 / BIG, OP.add)
+    ts(V("scc", 1, 2), V("scc", 3, 4), 4.0 - 4.0 / BIG, OP.mult, 4.0 / BIG, OP.add)
+    ts(V("scc", 2, 3), V("scc", 3, 4), 0.5 - 0.5 * BIG, OP.mult, 0.5 * BIG, OP.add)
+    ts(odd("w0"), V("cc"), 0.5, OP.mult)
+    copy(V("ftab"), col("fl32", 0, K))
+    for b in range(4): ts(col("f4", b, K), col("fl32", 0, K), 4.0, OP.mult, float(b), OP.add)
     quant(V("uq"), V("us"), V("ut"))
+    quant(*E(0), V("eb", 4, 516))
     do("v", lambda: g.vector.tensor_copy(T.urq[:, :].bitcast(dt.uint32), T.uq[:, :].bitcast(dt.uint32).indirect(T.uoff[:, 0:8])), [V("uq"), V("uoff")], [V("urq")])
-    pick("s", V("urs"), V("us"), V("uoff"))
-    pick("s", V("frow", 0, C), iota_win, V("ftab"))
-
-    def col(name, n): return V(name, C * n, C * n + C)
-    def E(b): return V("ebq", 128 * b, 128 * b + 128), V("ebs", 128 * b, 128 * b + 128)
-    def W(b): return V("wq", 128 * b, 128 * b + 128), V("wss", 128 * b, 128 * b + 128)
-    def bit_of(name, b): return V(name, b, 4 * C, 4)
+    pick("s", V("urs"), V("us"), V("uoff"), 0, 128)
+    pick("s", col("frow", 0), iota_win, V("ftab"))
+    for b in range(1, 4): quant(*E(b), V("eb", 4 - b, 516 - b))
 
     for n in range(3):
         qx, sx = col("qx", n), col("sx", n)
         cur, nxt = n % 2, (n + 1) % 2
-        frow, invf = col("frow", cur), V("inv", K * cur, K * cur + K)
-        mlist, bt = V("msg", 2 * K * n, 2 * K * n + K), V("msg", 2 * K * n + K, 2 * K * n + 2 * K)
+        frow, invf, invr = col("frow", cur), col("inv", cur, K), col("inv", nxt, K)
+        msg = col("msg", n, 2 * K)
+        bt = V("msg", msg[1] + 1, msg[2], 2)
+        gaps = []
+        if n:
+            gaps = [lambda: table(col("fl32", n, K), V("rsc")), lambda: send(partner[n], V("le%d" % n), col("fl32", n, K), "ae%d" % n)]
+            gaps += [lambda b=b: table(col("f4", b, K), V("rsc"), 1, 4.0 * MID + b + 0.25) for b in range(4)]
+            diag(V("rsc"), frow)
         quant2("qx", "sx", C * n, "xt")
-        mm(0, 0, B, V("urq"), V("urs"), V("qx", C * n, C * n + B), V("sx", C * n, C * n + B))
-        mm(1, 0, C - B, V("urq"), V("urs"), V("qx", C * n + B, C * n + C), V("sx", C * n + B, C * n + C))
+        mm(0, 0, B, V("urq"), V("urs"), part(qx, 0, B), part(sx, 0, B))
+        mm(1, 0, C - B, V("urq"), V("urs"), part(qx, B, C), part(sx, B, C))
         act(V("brow", B, C), V("ps1", 0, C - B), func=ACT.Sign)
+        some(gaps, 4)
         ts(V("brow", 0, B), V("ps0", 0, B), 0.0, OP.is_gt)
-        if n: diag(V("rsc"), frow)
+        some(gaps, 1)
         diag(V("bsc"), V("brow"))
-        if n: ts(mlist, V("rsc", 15, C, 16), T.scc[:, 0:1], OP.mult, extra=[V("scc")])
-        ts(bt, V("bsc", 15, C, 16), T.scc[:, 0:1], OP.mult, 0.5, OP.is_gt, extra=[V("scc")])
-        if n: send(partner[n], V("lb%d" % n), V("msg", 2 * K * n, 2 * K * n + 2 * K), "ab%d" % n)
-        else: send(partner[n], V("lb0"), bt, "ab0")
+        some(gaps)
+        ts(bt, V("bsc", 15, C, 16), T.scc[:, 2:3], OP.is_gt, 0.5, OP.subtract, extra=[V("scc")])
+        send(partner[n], V("lb%d" % n), msg, "ab%d" % n)
         send(partner[n], V("lc%d" % n), qx, "ac%d" % n, codes=True)
         send(partner[n], V("lp%d" % n), sx, "ap%d" % n)
-        if n:
-            for b in range(4): table(V("f4", K * b, K * b + K), V("rsc"), 1, 4.0 * MID + b + 0.25)
-        for b in range(4): mm(4 + b, 0, C, *E(b), qx, sx)
-        for b in (0, 1): pick("s", bit_of("xp", b), V("xt"), V("f4", K * b, K * b + K))
-        for b in (2, 3): pick("v", bit_of("xp", b), V("xt"), V("f4", K * b, K * b + K))
-        quant(V("qp"), V("sp"), V("xp"))
-        def halves(out, bank):
-            todo = [(b, h) for b in range(4) for h in range(2)]
-            def some(k):
-                for b, h in todo[:k]: act(V(out, C * b + H * h, C * b + H * h + H), V("ps%d" % (bank + b), H * h, H * h + H))
-                del todo[:k]
-            return some
-        numbers, sums = halves("fh", 4), halves("gs", 0)
-        numbers(4)
-        for b in range(4): mm(b, 0, C, *E(b), V("qp"), V("sp"), True, False)
-        if n == 0:
-            lay(V("ainv"), V("ftab"), iota_win)
-            diag(V("isc"), V("ainv"))
-            table(invf, V("isc"))
-        le = V("lb%d" % n, 0, K) if n else V("le0")
-        lb = V("lb%d" % n, K, 2 * K) if n else V("lb0")
-        tt(V("dif"), V("cc"), le, OP.subtract)
-        tt(V("gate"), bt, lb, OP.not_equal)
-        tt(V("w1"), V("gate"), V("dif"), OP.mult)
-        tt(V("w2"), V("w1"), le, OP.add)
-        tab = [V("tab", K * i, K * i + K) for i in range(2)]
-        row = [col("row", i) for i in range(2)]
-        ts(tab[0], V("w2"), MID + 0.25, OP.add)
-        for b in range(4): mm(b, 0, C, *E(b), V("lc%d" % n), V("lp%d" % n), False, True)
-        spare = [lambda: ts(V("w3"), V("gate"), -float(C), OP.mult, C + MID + 0.25, OP.add), lambda: tt(V("w4"), V("cc"), V("w1"), OP.subtract),
-                 lambda: tt(V("w4"), V("w3"), V("w4"), OP.add), lambda: copy(V("fin"), V("w4"))]
+        for b in range(3): mm(4 + b, 0, C, *E(b), qx, sx)
+        def halves(call, out, bank, count):
+            return [lambda b=b, h=h: call(V(out, C * b + H * h, C * b + H * h + H), V("ps%d" % (bank + b), H * h, H * h + H)) for b in range(count) for h in range(2)]
+        own_v = OWN_V if n else 0
+        numbers_v, numbers, sums = halves(copy, "fh", 4, 3)[:own_v], halves(act, "fh", 4, 3)[own_v:], halves(act, "gs", 0, 4)
+        ahead = [lambda: tt(even("w0"), V("le%d" % n), V("cc"), OP.subtract), lambda: scan(V("w1"), V("mq"), V("w0")),
+                 lambda: ts(V("w3"), even("w0"), -1.0, OP.mult, float(C), OP.add), lambda: ts(odd("w2"), odd("w1"), 0.25 * C, OP.add),
+                 lambda: tt(even("w1"), even("w1"), bt, OP.mult), lambda: tt(even("w2"), V("w3"), bt, OP.mult)]
+        xs = XP_S if n else 4
+        for b in range(4): pick("s" if b < xs else "v", bit_of("xp", b), V("xt"), col("f4", b, K))
+        if n == 0: lay(V("ainv"), V("ftab"), iota_win)
+        some(numbers_v, 1)
+        some(ahead, 1)
+        some(numbers_v, 1)
+        some(ahead, 2)
+        some(numbers_v)
+        some(ahead)
+        some(numbers, len(numbers) - (OWN_T if n else 6))
+        spare = [lambda a=a: quant2("qp", "sp", 0, "xp", [(a, a + 128)]) for a in (0, 128, 256)]
+        if n == 0: spare += [lambda: diag(V("isc"), V("ainv")), lambda: table(invf, V("isc"))]
+        scan(V("t1"), V("lb%d" % n), V("w1"))
+        scan(V("t2"), V("lb%d" % n), V("w2"))
+        tab, row = [col("tab", i, K) for i in range(2)], [col("row", i) for i in range(2)]
+        ts(tab[0], odd("t1"), 2.0, OP.mult)
+        ts(V("fin"), odd("t2"), 2.0, OP.mult)
         pick2(row[0], iota_win, tab[0])
-        for lv in range(1, 8):
-            o, w = (lv - 1) % 2, lv % 2
-            pick2(row[w], row[o], tab[o])
-            numbers(OWN_SLOTS.get(lv, 0))
-            sums(SUM_SLOTS.get(lv, 0))
-            diag(V("scan"), row[w])
-            if spare: spare.pop(0)()
-            table(tab[w], V("scan"))
-        pick2(row[0], row[1], tab[1])
-        pick2(V("wi", 0, C), row[0], tab[1])
+        for i, step in enumerate(STEPS):
+            if step == "P":
+                pick2(V("wi", 0, C) if i == len(STEPS) - 1 else row[1], row[0], tab[0])
+                some(spare, 1)
+                if i == 6:
+                    for b in range(4): mm(b, 0, C, *E(b), V("qp"), V("sp"), True, False)
+                    for b in range(4): mm(b, 0, C, *E(b), V("lc%d" % n), V("lp%d" % n), False, True)
+                row.reverse()
+                continue
+            if step == "F": pick("s", row[1], row[0], tab[0], HELP, C)
+            else:
+                some(numbers, 2 if step == "T" else 0)
+                some(sums, int(step[1:] or 0))
+            diag(V("scan"), row[0])
+            if step == "F":
+                if HELP: pick("v", row[1], row[0], tab[0], 0, HELP)
+                row.reverse()
+            table(tab[1], V("scan"))
+            tab.reverse()
         pick2(V("arow"), V("wi"), V("fin"))
-        sums(8)
+        some(numbers)
+        some(sums)
         diag(V("scan"), V("arow"))
         at = V("atab")
         table(at, V("scan"))
@@ -274,35 +311,35 @@ def rank_program(g, core, T, topo):
         quant2("qz", "sz", 0, "zt")
         mm(4, 0, B, *W(0), V("qz", 0, B), V("sz", 0, B))
         mm(0, 0, C - B, *W(0), V("qz", B, C), V("sz", B, C))
-        for b in range(1, 4): mm(4 + b, 0, C, *W(b), V("qz"), V("sz"))
+        for b in (1, 3, 2): mm(4 + b, 0, C, *W(b), V("qz"), V("sz"))
         mm(3, 0, C, *E(3), qx, sx)
-        if n == 1: quant(V("vq"), V("vs"), V("vt"))
         pick("s", V("ginv"), V("ainv"), invf)
+        pick("s", col("frow", nxt), frow, at, 0, H)
         diag(V("isc"), V("ginv"))
         ts(V("pc", 0, B), V("ps4", 0, B), 2.0 ** -6, OP.mult)
-        invr = V("inv", K * nxt, K * nxt + K)
         table(invr, V("isc"))
+        if n == 1: quant(V("vq"), V("vs"), V("vt"))
         act(V("pc", B, C), V("ps0", 0, C - B), scale=2.0 ** -6)
-        for b in range(1, 4): act(col("pc", b), V("ps%d" % (4 + b), 0, C), scale=2.0 ** -6)
-        pick("s", V("p3"), col("pc", 3), invr)
-        pick("s", col("frow", nxt), frow, at)
-        for b in range(3): pickadd(bit_of("xt", b), col("pc", b), invr, col("fh", b))
-        tt(bit_of("xt", 3), V("ps3", 0, C), V("p3"), OP.add)
-
-    def store(q, dst, in_, sem, codes=False, a=None):
-        src = a if a is not None else (ap(in_).bitcast(dt.uint8) if codes else ap(in_))
-        do(q, lambda: queue[q].dma_start(dst, src), [in_], [], sem=sem, n=16)
-    quant2("qx", "sx", 3 * C, "xt")
-    do("s", lambda: g.scalar.activation(T.lnf[:, :], ap(col("frow", 1)), ACT.Identity, bias=float(MID)), [col("frow", 1)], [V("lnf")])
-    store("y", T.oc[:, :], col("qx", 3), "oc", codes=True)
-    for b in range(2):
-        mm(b, 0, H, V("vq"), V("vs"), V("qx", 3 * C + H * b, 3 * C + H * b + H), V("sx", 3 * C + H * b, 3 * C + H * b + H))
+        for b in (1, 3, 2): act(col("pc", b), V("ps%d" % (4 + b), 0, C), scale=2.0 ** -6)
+        pieces = ((0, B), (B, C)) if n == 2 and TAIL else ((0, C),)
+        for a, e in pieces: pick("s", V("p3"), col("pc", 3), invr, a, e)
+        pick("s", col("frow", nxt), frow, at, H, C)
+        for k, (a, e) in enumerate(pieces):
+            for b in range(3): pickadd(bit_of("xt", b), col("pc", b), invr, col("fh", b), a, e)
+            tt(part(bit_of("xt", 3), a, e), V("ps3", a, e), V("p3", a, e), OP.add)
+            if n == 2 and TAIL:
+                q, s = part(col("qx", 3), a, e), part(col("sx", 3), a, e)
+                quant(q, s, V("xt", 4 * a, 4 * e))
+                store("y", T.oc[:, 4 * a:4 * e], q, "oc%d" % k, codes=True)
+                mm(k, 0, e - a, V("vq"), V("vs"), q, s)
+                if k == 0:
+                    act(V("ysb", a, e), V("ps0", 0, e - a))
+                    store("s", T.y[:, a:e], V("ysb", a, e), "oy0")
+                    do("s", lambda: g.scalar.activation(T.lnf[:, :], ap(col("frow", 1)), ACT.Identity, bias=float(MID)), [col("frow", 1)], [V("lnf")])
+                    store("s", T.ln[:, :], V("lnf"), "ol", a=T.lnf[0:128:16, :])
     for k in range(4):
         store("y" if k < 2 else "s", T.osc[4 * k:4 * k + 4, :], col("sx", 3), "os%d" % k, a=T.sx[32 * k:32 * k + 4, 3 * C:4 * C])
-    copy(V("ysb", 0, H), V("ps0", 0, H))
-    act(V("ysb", H, C), V("ps1", 0, H))
-    store("y", T.y[:, 0:H], V("ysb", 0, H), "oy0")
-    store("s", T.y[:, H:C], V("ysb", H, C), "oy1")
-    store("y", T.ln[:, :], V("lnf"), "ol", a=T.lnf[0:128:16, :])
+    copy(V("ysb", B, C), V("ps1", 0, C - B))
+    store("y", T.y[:, B:C], V("ysb", B, C), "oy1")
     for s in sorted(total):
         wait("g", (s, total[s]))

@@ -14,7 +14,7 @@ def _buffers(where, kind, **widths):
 _buffers("sbuf", "bfloat16", wi=2 * C, m16=16, msk=C, eb0=520, eb=520, ut=512, vt=512, xt=4 * C, xp=4 * C, zt=4 * C, fh=4 * C,
          brow=C, bsc=C, msg=6 * K, row=2 * C, scan=C, arow=C, ainv=C, ginv=C, isc=C, frow=2 * C, rsc=C, mq=2 * K, lb0=2 * K, lb1=2 * K, lb2=2 * K)
 _buffers("sbuf", "int32", dmod=16, dmod2=16, pt=K, pt2=K, st=K, ui=8, fl32=3 * K, le0=K, le1=K, le2=K)
-_buffers("sbuf", "float32", m1=16, m2=16, cc=K, scc=4, gs=4 * C, pc=4 * C, p3=C, w0=2 * K, w1=2 * K, w2=2 * K, w3=K, t1=2 * K, t2=2 * K, lnf=C, ysb=C)
+_buffers("sbuf", "float32", m1=16, m2=16, cc=K, scc=4, gs=4 * C, pc=4 * C, p3=4 * C, w0=2 * K, w1=2 * K, w2=2 * K, w3=K, t1=2 * K, t2=2 * K, lnf=C, ysb=C)
 _buffers("sbuf", "uint16", poff=K, uoff=8, tab=2 * K, fin=K, atab=K, inv=2 * K, ftab=K, f4=4 * K)
 _buffers("sbuf", "float8_e4m3fn_x4", ebq=512, uq=128, urq=128, vq=128, wq=512, qx=4 * C, qp=C, qz=C, lc0=C, lc1=C, lc2=C)
 _buffers("sbuf", "uint8", ebs=512, us=128, urs=128, vs=128, wss=512, sx=4 * C, sp=C, sz=C, lp0=C, lp1=C, lp2=C)
@@ -24,12 +24,20 @@ SEMAPHORES = ["cv", "cs", "ct", "cg", "sent"]
 SEMAPHORES += ["%s%d" % (_k, _n) for _k in ("ae", "ab", "ac", "ap") for _n in range(3)]
 SEMAPHORES += ["dx", "dx2", "du", "dv", "df", "dw", "dws", "oy0", "oy1", "ol", "oc0", "oc1", "os0", "os1", "os2", "os3"]
 
-STEPS = ["P", "T", "P", "T", "P", "T", "P", "T", "P", "T", "P", "T2", "P", "T3", "P", "P"]
+STEPS = ["P", "F", "P", "F", "P", "F", "P", "F", "P", "T2", "P", "T3", "P", "P"]
 HELP = 96
-OWN_V = 0
+OWN_V = 2
 XP_S = 3
-OWN_T = 6
-TAIL = 1
+OWN_T = 2
+QSH = 0
+GAPV = 1
+BACK_V = "0C 1C 2A 3A 3B qA 2B r qB"
+LAST_V = "0A 1A 2A 3A qA 0B 1B 3B 2B qB"
+BACK_S = "3C 2B R"
+CORD = (1, 3, 2)
+RH = 192
+G1 = 4
+G2 = 1
 
 
 def rank_program(g, core, T, topo):
@@ -240,15 +248,16 @@ def rank_program(g, core, T, topo):
         if n:
             gaps = [lambda: table(col("fl32", n, K), V("rsc")), lambda: send(partner[n], V("le%d" % n), col("fl32", n, K), "ae%d" % n)]
             gaps += [lambda b=b: table(col("f4", b, K), V("rsc"), 1, 4.0 * MID + b + 0.25) for b in range(4)]
-            diag(V("rsc"), frow)
-        quant2("qx", "sx", C * n, "xt")
-        mm(0, 0, B, V("urq"), V("urs"), part(qx, 0, B), part(sx, 0, B))
-        mm(1, 0, C - B, V("urq"), V("urs"), part(qx, B, C), part(sx, B, C))
-        act(V("brow", B, C), V("ps1", 0, C - B), func=ACT.Sign)
-        some(gaps, 4)
-        ts(V("brow", 0, B), V("ps0", 0, B), 0.0, OP.is_gt)
-        some(gaps, 1)
-        diag(V("bsc"), V("brow"))
+        if n == 0:
+            quant2("qx", "sx", 0, "xt")
+            mm(4, 0, B, V("urq"), V("urs"), part(qx, 0, B), part(sx, 0, B))
+            act(V("brow", 0, B), V("ps4", 0, B), func=ACT.Sign)
+        mm(5, 0, C - B, V("urq"), V("urs"), part(qx, B, C), part(sx, B, C))
+        act(V("brow", B, C), V("ps5", 0, C - B), func=ACT.Sign)
+        some(gaps, G1)
+        scan(V("bsc", 0, B), V("msk", 0, B), V("brow", 0, B))
+        some(gaps, G2)
+        scan(V("bsc", B, C), V("msk", B, C), V("brow", B, C))
         some(gaps)
         ts(bt, V("bsc", 15, C, 16), T.scc[:, 2:3], OP.is_gt, 0.5, OP.subtract, extra=[V("scc")])
         send(partner[n], V("lb%d" % n), msg, "ab%d" % n)
@@ -273,6 +282,10 @@ def rank_program(g, core, T, topo):
         some(ahead)
         some(numbers, len(numbers) - (OWN_T if n else 6))
         spare = [lambda a=a: quant2("qp", "sp", 0, "xp", [(a, a + 128)]) for a in (0, 128, 256)]
+        if n and QSH: some(spare)
+        left = (OWN_T if n else 6) // 2 if GAPV else 0
+        spare2 = [lambda b=b, a=a: copy(V("fh", C * b + a, C * b + a + 128), V("ps%d" % (4 + b), a, a + 128)) for b in range(3 - left, 3) for a in (0, 128, 256)]
+        if left: del numbers[:]
         if n == 0: spare += [lambda: diag(V("isc"), V("ainv")), lambda: table(invf, V("isc"))]
         scan(V("t1"), V("lb%d" % n), V("w1"))
         scan(V("t2"), V("lb%d" % n), V("w2"))
@@ -283,7 +296,7 @@ def rank_program(g, core, T, topo):
         for i, step in enumerate(STEPS):
             if step == "P":
                 pick2(V("wi", 0, C) if i == len(STEPS) - 1 else row[1], row[0], tab[0])
-                some(spare, 1)
+                some(spare or spare2, 1)
                 if i == 6:
                     for b in range(4): mm(b, 0, C, *E(b), V("qp"), V("sp"), True, False)
                     for b in range(4): mm(b, 0, C, *E(b), V("lc%d" % n), V("lp%d" % n), False, True)
@@ -299,8 +312,10 @@ def rank_program(g, core, T, topo):
                 row.reverse()
             table(tab[1], V("scan"))
             tab.reverse()
+            some(spare2, 1)
         pick2(V("arow"), V("wi"), V("fin"))
         some(numbers)
+        some(spare2)
         some(sums)
         diag(V("scan"), V("arow"))
         at = V("atab")
@@ -311,35 +326,49 @@ def rank_program(g, core, T, topo):
         quant2("qz", "sz", 0, "zt")
         mm(4, 0, B, *W(0), V("qz", 0, B), V("sz", 0, B))
         mm(0, 0, C - B, *W(0), V("qz", B, C), V("sz", B, C))
-        for b in (1, 3, 2): mm(4 + b, 0, C, *W(b), V("qz"), V("sz"))
-        mm(3, 0, C, *E(3), qx, sx)
+        for b in CORD: mm(4 + b, 0, C, *W(b), V("qz"), V("sz"))
+        by_s = BACK_S.split()
+        for b in (3, 2, 1):
+            if any(w[0] == str(b) for w in by_s): mm(b, 0, C, *E(b), qx, sx)
         pick("s", V("ginv"), V("ainv"), invf)
-        pick("s", col("frow", nxt), frow, at, 0, H)
+        pick("s", col("frow", nxt), frow, at, 0, RH)
         diag(V("isc"), V("ginv"))
         ts(V("pc", 0, B), V("ps4", 0, B), 2.0 ** -6, OP.mult)
         table(invr, V("isc"))
         if n == 1: quant(V("vq"), V("vs"), V("vt"))
         act(V("pc", B, C), V("ps0", 0, C - B), scale=2.0 ** -6)
-        for b in (1, 3, 2): act(col("pc", b), V("ps%d" % (4 + b), 0, C), scale=2.0 ** -6)
-        pieces = ((0, B), (B, C)) if n == 2 and TAIL else ((0, C),)
-        for a, e in pieces: pick("s", V("p3"), col("pc", 3), invr, a, e)
-        pick("s", col("frow", nxt), frow, at, H, C)
-        for k, (a, e) in enumerate(pieces):
-            for b in range(3): pickadd(bit_of("xt", b), col("pc", b), invr, col("fh", b), a, e)
-            tt(part(bit_of("xt", 3), a, e), V("ps3", a, e), V("p3", a, e), OP.add)
-            if n == 2 and TAIL:
-                q, s = part(col("qx", 3), a, e), part(col("sx", 3), a, e)
+        for b in CORD: act(col("pc", b), V("ps%d" % (4 + b), 0, C), scale=2.0 ** -6)
+        piece = {"A": (0, B), "B": (B, C), "C": (0, C)}
+        for w in by_s:
+            if w == "R": pick("s", col("frow", nxt), frow, at, RH, C)
+            else: pick("s", col("p3", int(w[0])), col("pc", int(w[0])), invr, *piece[w[1]])
+        for w in (BACK_V if n < 2 else LAST_V).split():
+            if w == "r":
+                diag(V("rsc"), col("frow", nxt))
+                continue
+            a, e = piece[w[1]]
+            if w[0] == "q":
+                q, s = part(col("qx", n + 1), a, e), part(col("sx", n + 1), a, e)
                 quant(q, s, V("xt", 4 * a, 4 * e))
-                store("y", T.oc[:, 4 * a:4 * e], q, "oc%d" % k, codes=True)
-                mm(k, 0, e - a, V("vq"), V("vs"), q, s)
-                if k == 0:
-                    act(V("ysb", a, e), V("ps0", 0, e - a))
-                    store("s", T.y[:, a:e], V("ysb", a, e), "oy0")
-                    do("s", lambda: g.scalar.activation(T.lnf[:, :], ap(col("frow", 1)), ACT.Identity, bias=float(MID)), [col("frow", 1)], [V("lnf")])
-                    store("s", T.ln[:, :], V("lnf"), "ol", a=T.lnf[0:128:16, :])
+                k = int(w[1] == "B")
+                if n == 2:
+                    store("y", T.oc[:, 4 * a:4 * e], q, "oc%d" % k, codes=True)
+                    mm(4 + k, 0, e - a, V("vq"), V("vs"), q, s)
+                    if k == 0:
+                        act(V("ysb", a, e), V("ps4", 0, e - a))
+                        store("s", T.y[:, a:e], V("ysb", a, e), "oy0")
+                        do("s", lambda: g.scalar.activation(T.lnf[:, :], ap(col("frow", 1)), ACT.Identity, bias=float(MID)), [col("frow", 1)], [V("lnf")])
+                        store("s", T.ln[:, :], V("lnf"), "ol", a=T.lnf[0:128:16, :])
+                elif k == 0:
+                    mm(4, 0, B, V("urq"), V("urs"), q, s)
+                    act(V("brow", 0, B), V("ps4", 0, B), func=ACT.Sign)
+                continue
+            b = int(w[0])
+            if w in by_s or w[0] + "C" in by_s: tt(part(bit_of("xt", b), a, e), V("ps%d" % b, a, e), part(col("p3", b), a, e), OP.add)
+            else: pickadd(bit_of("xt", b), col("pc", b), invr, col("fh", b), a, e)
     for k in range(4):
         store("y" if k < 2 else "s", T.osc[4 * k:4 * k + 4, :], col("sx", 3), "os%d" % k, a=T.sx[32 * k:32 * k + 4, 3 * C:4 * C])
-    copy(V("ysb", B, C), V("ps1", 0, C - B))
+    copy(V("ysb", B, C), V("ps5", 0, C - B))
     store("y", T.y[:, B:C], V("ysb", B, C), "oy1")
     for s in sorted(total):
         wait("g", (s, total[s]))

@@ -11,10 +11,11 @@ BIG = 2.0 ** 22
 SCRATCH = {}
 def _buffers(where, kind, **widths):
     for name, width in widths.items(): SCRATCH[name] = (where, [128, width], kind)
-_buffers("sbuf", "bfloat16", wi=2 * C, m16=16, msk=C, eb0=520, eb=520, ut=512, vt=512, xt=4 * C, xp=4 * C, zt=4 * C, fh=4 * C,
-         brow=C, bsc=C, msg=6 * K, row=2 * C, scan=C, arow=C, ainv=C, ginv=C, isc=C, frow=2 * C, rsc=C, mq=2 * K, lb0=2 * K, lb1=2 * K, lb2=2 * K)
-_buffers("sbuf", "int32", dmod=16, dmod2=16, pt=K, pt2=K, st=K, ui=8, fl32=3 * K, le0=K, le1=K, le2=K)
-_buffers("sbuf", "float32", m1=16, m2=16, cc=K, scc=4, gs=4 * C, pc=4 * C, p3=4 * C, w0=2 * K, w1=2 * K, w2=2 * K, w3=K, t1=2 * K, t2=2 * K, lnf=C, ysb=C)
+_buffers("sbuf", "bfloat16", wi=2 * C, m16=16, msk=C, eb0=520, eb=520, ut=512, vt=512, xt=4 * C, xp=4 * C, zt=4 * C, fh=3 * C,
+         brow=C, bsc=C, msg=6 * K, row=2 * C, scan=C, arow=C, ainv=C, ginv=C, isc=C, frow=2 * C, rsc=C, lb0=2 * K, lb1=2 * K, lb2=2 * K)
+_buffers("sbuf", "int32", dmod=16, dmod2=16, pt=K, pt2=K, st=K, ui=8, fl32=K)
+_buffers("sbuf", "float32", m1=16, m2=16, cc=K, ca=K, cb=K, scc=8, gs=4 * C, pc=4 * C, p3=4 * C, w1=2 * K, w2=2 * K, w3=K, w4=K, w5=K, t1=2 * K, t2=2 * K,
+         fq=3 * K, le0=K, le1=K, le2=K, lnf=C, ysb=C)
 _buffers("sbuf", "uint16", poff=K, uoff=8, tab=2 * K, fin=K, atab=K, inv=2 * K, ftab=K, f4=4 * K)
 _buffers("sbuf", "float8_e4m3fn_x4", ebq=512, uq=128, urq=128, vq=128, wq=512, qx=4 * C, qp=C, qz=C, lc0=C, lc1=C, lc2=C)
 _buffers("sbuf", "uint8", ebs=512, us=128, urs=128, vs=128, wss=512, sx=4 * C, sp=C, sz=C, lp0=C, lp1=C, lp2=C)
@@ -24,18 +25,17 @@ SEMAPHORES = ["cv", "cs", "ct", "cg", "sent"]
 SEMAPHORES += ["%s%d" % (_k, _n) for _k in ("ae", "ab", "ac", "ap") for _n in range(3)]
 SEMAPHORES += ["dx", "dx2", "du", "dv", "df", "dw", "dws", "oy0", "oy1", "ol", "oc0", "oc1", "os0", "os1", "os2", "os3"]
 
-STEPS = ["P", "F", "P", "F", "P", "F", "P", "F", "P", "T2", "P", "T3", "P", "P"]
-HELP = 96
-OWN_V = 2
+STEPS = ["P", "F"] * 6 + ["P"]
+HELP = 128
+OWN = ((0, 0), (3, 0))
 XP_S = 3
-OWN_T = 2
-QSH = 0
-GAPV = 1
-BACK_V = "0C 1C 2A 3A 3B qA 2B r qB"
-LAST_V = "0A 1A 2A 3A qA 0B 1B 3B 2B qB"
-BACK_S = "3C 2B R"
+BACK_V = "0C 1C 2A 3A 2B qA 3B r qB"
+LAST_V = "0A 1A 2A 3A qA 0B 1B 2B 3B qB"
+BACK_S = "3A 3B R"
 CORD = (1, 3, 2)
-RH = 192
+RH = 128
+SV0 = 10
+SS0 = 11
 G1 = 4
 G2 = 1
 
@@ -155,8 +155,8 @@ def rank_program(g, core, T, topo):
         out = V("ps%d" % bank, a, b)
         do("t", lambda: g.tensor.matmul_mx(ap(out), ap(wq), ap(ws), ap(xq), ap(xs), start, stop), [wq, ws, xq, xs], [out], joins=not start)
 
-    def diag(sc, row):
-        scan(sc, V("msk"), row)
+    def diag(sc, row, a=0, b=C):
+        scan(part(sc, a, b), V("msk", a, b), part(row, a, b))
 
     def table(out, sc, mul=0, add=MID + 0.25):
         ts(out, V(sc[0], 15, C, 16), T.scc[:, mul:mul + 1], OP.mult, add, OP.add, extra=[V("scc")])
@@ -193,7 +193,7 @@ def rank_program(g, core, T, topo):
         for k, s in (("le", "ae"), ("lb", "ab"), ("lc", "ac"), ("lp", "ap")):
             arrives("%s%d" % (k, n), "%s%d" % (s, n), partner[n])
 
-    load("s", col("fl32", 0, K), T.fl[:, :], "df")
+    load("s", V("fl32"), T.fl[:, :], "df")
     load("y", V("ut"), T.u[:, :], "du")
     load("y", V("xt", 0, 4 * B), T.x[:, 0:4 * B], "dx")
     load("y", V("xt", 4 * B, 4 * C), T.x[:, 4 * B:4 * C], "dx2")
@@ -210,33 +210,32 @@ def rank_program(g, core, T, topo):
     iota(V("ui"), [[16, 8]], 0, 0)
     iota(V("st"), [[16, K]], 0, 0)
     do("g", lambda: g.affine_select(T.eb[:, :], T.eb0[:, :], [[1, 520]], OP.is_equal, 0.0, -4, -4), [V("eb0")], [V("eb")])
-    send(partner[0], V("le0"), col("fl32", 0, K), "ae0")
     fill(V("msg"), 0.0)
-    scan(iota_win, V("eb0", 0, C), V("eb0", 0, C), -MID - 1.0, OP.add)
     ts(V("dmod2"), V("dmod"), 15, OP.bitwise_and)
+    scan(iota_win, V("eb0", 0, C), V("eb0", 0, C), -MID - 1.0, OP.add)
     ts(V("pt2"), V("pt"), 15, OP.bitwise_and)
     ts(V("m1"), V("dmod2"), 1.0, OP.is_equal, BIG - 1.0, OP.mult)
     ts(V("m2"), V("dmod2"), 0.0, OP.not_equal)
-    copy(V("poff"), V("pt2"))
     copy(V("uoff"), V("ui"))
+    copy(V("poff"), V("pt2"))
+    ts(V("scc", 7, 8), V("pt2", 0, 1), 15.0, OP.is_equal)
     tt(V("m16"), V("m1"), V("m2"), OP.add)
-    tt(V("cc"), V("pt2"), V("st"), OP.add)
-    ts(V("scc", 3, 4), V("pt2", 0, 1), 15.0, OP.is_equal)
     pick("s", V("msk"), V("m16"), V("poff"))
-    fill(even("mq"), 0.0)
-    fill(odd("mq"), 0.25)
-    ts(V("scc", 0, 1), V("scc", 3, 4), 1.0 - 1.0 / BIG, OP.mult, 1.0 / BIG, OP.add)
-    ts(V("scc", 1, 2), V("scc", 3, 4), 4.0 - 4.0 / BIG, OP.mult, 4.0 / BIG, OP.add)
-    ts(V("scc", 2, 3), V("scc", 3, 4), 0.5 - 0.5 * BIG, OP.mult, 0.5 * BIG, OP.add)
-    ts(odd("w0"), V("cc"), 0.5, OP.mult)
-    copy(V("ftab"), col("fl32", 0, K))
-    for b in range(4): ts(col("f4", b, K), col("fl32", 0, K), 4.0, OP.mult, float(b), OP.add)
+    tt(V("cc"), V("pt2"), V("st"), OP.add)
+    for i, (last, others) in enumerate(((1.0, 1.0 / BIG), (4.0, 4.0 / BIG), (0.5, 0.5 * BIG), (0.25, 0.25 / BIG))):
+        ts(V("scc", i, i + 1), V("scc", 7, 8), last - others, OP.mult, others, OP.add)
+    ts(V("ca"), V("cc"), 0.25, OP.mult)
+    ts(V("cb"), V("cc"), 0.25, OP.mult, 0.25 * C, OP.add)
+    ts(col("fq", 0, K), V("fl32"), 0.25, OP.mult)
+    send(partner[0], V("le0"), col("fq", 0, K), "ae0")
+    copy(V("ftab"), V("fl32"))
+    four = [lambda b=b: ts(col("f4", b, K), V("fl32"), 4.0, OP.mult, float(b), OP.add) for b in range(4)]
+    some(four, 1)
     quant(V("uq"), V("us"), V("ut"))
-    quant(*E(0), V("eb", 4, 516))
+    some(four)
     do("v", lambda: g.vector.tensor_copy(T.urq[:, :].bitcast(dt.uint32), T.uq[:, :].bitcast(dt.uint32).indirect(T.uoff[:, 0:8])), [V("uq"), V("uoff")], [V("urq")])
     pick("s", V("urs"), V("us"), V("uoff"), 0, 128)
     pick("s", col("frow", 0), iota_win, V("ftab"))
-    for b in range(1, 4): quant(*E(b), V("eb", 4 - b, 516 - b))
 
     for n in range(3):
         qx, sx = col("qx", n), col("sx", n)
@@ -244,104 +243,101 @@ def rank_program(g, core, T, topo):
         frow, invf, invr = col("frow", cur), col("inv", cur, K), col("inv", nxt, K)
         msg = col("msg", n, 2 * K)
         bt = V("msg", msg[1] + 1, msg[2], 2)
-        gaps = []
         if n:
-            gaps = [lambda: table(col("fl32", n, K), V("rsc")), lambda: send(partner[n], V("le%d" % n), col("fl32", n, K), "ae%d" % n)]
+            gaps = [lambda: table(col("fq", n, K), V("rsc"), 3, 0.25 * MID), lambda: send(partner[n], V("le%d" % n), col("fq", n, K), "ae%d" % n)]
             gaps += [lambda b=b: table(col("f4", b, K), V("rsc"), 1, 4.0 * MID + b + 0.25) for b in range(4)]
-        if n == 0:
+        else:
+            gaps = [lambda b=b: quant(*E(b), V("eb", 4 - b, 516 - b)) for b in range(4)]
             quant2("qx", "sx", 0, "xt")
             mm(4, 0, B, V("urq"), V("urs"), part(qx, 0, B), part(sx, 0, B))
             act(V("brow", 0, B), V("ps4", 0, B), func=ACT.Sign)
         mm(5, 0, C - B, V("urq"), V("urs"), part(qx, B, C), part(sx, B, C))
         act(V("brow", B, C), V("ps5", 0, C - B), func=ACT.Sign)
         some(gaps, G1)
-        scan(V("bsc", 0, B), V("msk", 0, B), V("brow", 0, B))
+        diag(V("bsc"), V("brow"), 0, B)
         some(gaps, G2)
-        scan(V("bsc", B, C), V("msk", B, C), V("brow", B, C))
+        diag(V("bsc"), V("brow"), B, C)
         some(gaps)
         ts(bt, V("bsc", 15, C, 16), T.scc[:, 2:3], OP.is_gt, 0.5, OP.subtract, extra=[V("scc")])
         send(partner[n], V("lb%d" % n), msg, "ab%d" % n)
         send(partner[n], V("lc%d" % n), qx, "ac%d" % n, codes=True)
         send(partner[n], V("lp%d" % n), sx, "ap%d" % n)
         for b in range(3): mm(4 + b, 0, C, *E(b), qx, sx)
-        def halves(call, out, bank, count):
-            return [lambda b=b, h=h: call(V(out, C * b + H * h, C * b + H * h + H), V("ps%d" % (bank + b), H * h, H * h + H)) for b in range(count) for h in range(2)]
-        own_v = OWN_V if n else 0
-        numbers_v, numbers, sums = halves(copy, "fh", 4, 3)[:own_v], halves(act, "fh", 4, 3)[own_v:], halves(act, "gs", 0, 4)
-        ahead = [lambda: tt(even("w0"), V("le%d" % n), V("cc"), OP.subtract), lambda: scan(V("w1"), V("mq"), V("w0")),
-                 lambda: ts(V("w3"), even("w0"), -1.0, OP.mult, float(C), OP.add), lambda: ts(odd("w2"), odd("w1"), 0.25 * C, OP.add),
-                 lambda: tt(even("w1"), even("w1"), bt, OP.mult), lambda: tt(even("w2"), V("w3"), bt, OP.mult)]
+        def out_of(call, out, bank, count, w):
+            return [lambda b=b, a=a: call(V(out, C * b + a, C * b + a + w), V("ps%d" % (bank + b), a, a + w)) for b in range(count) for a in range(0, C, w)]
+        own_v, own_s = OWN[min(n, 1)]
+        numbers_v, numbers_s = out_of(copy, "fh", 4, 3, 128)[:own_v], out_of(act, "fh", 4, 3, 128)[own_v:]
+        sums_v, sums_s = out_of(copy, "gs", 0, 2, H), out_of(act, "gs", 0, 4, 128)[6:]
         xs = XP_S if n else 4
         for b in range(4): pick("s" if b < xs else "v", bit_of("xp", b), V("xt"), col("f4", b, K))
         if n == 0: lay(V("ainv"), V("ftab"), iota_win)
-        some(numbers_v, 1)
-        some(ahead, 1)
-        some(numbers_v, 1)
-        some(ahead, 2)
         some(numbers_v)
-        some(ahead)
-        some(numbers, len(numbers) - (OWN_T if n else 6))
+        some(numbers_s, own_s)
+        le = V("le%d" % n)
+        ts(V("w5"), bt, 4.0, OP.mult)
+        tt(V("w3"), le, V("ca"), OP.subtract)
+        tt(V("w4"), V("cb"), le, OP.subtract)
+        tt(odd("w1"), le, V("ca"), OP.add)
+        tt(odd("w2"), le, V("cb"), OP.add)
+        tt(even("w1"), V("w3"), V("w5"), OP.mult)
+        tt(even("w2"), V("w4"), V("w5"), OP.mult)
         spare = [lambda a=a: quant2("qp", "sp", 0, "xp", [(a, a + 128)]) for a in (0, 128, 256)]
-        if n and QSH: some(spare)
-        left = (OWN_T if n else 6) // 2 if GAPV else 0
-        spare2 = [lambda b=b, a=a: copy(V("fh", C * b + a, C * b + a + 128), V("ps%d" % (4 + b), a, a + 128)) for b in range(3 - left, 3) for a in (0, 128, 256)]
-        if left: del numbers[:]
         if n == 0: spare += [lambda: diag(V("isc"), V("ainv")), lambda: table(invf, V("isc"))]
         scan(V("t1"), V("lb%d" % n), V("w1"))
         scan(V("t2"), V("lb%d" % n), V("w2"))
         tab, row = [col("tab", i, K) for i in range(2)], [col("row", i) for i in range(2)]
-        ts(tab[0], odd("t1"), 2.0, OP.mult)
-        ts(V("fin"), odd("t2"), 2.0, OP.mult)
+        ts(tab[0], odd("t1"), 2.0, OP.mult, 0.25, OP.add)
+        ts(V("fin"), odd("t2"), 2.0, OP.mult, 0.25, OP.add)
         pick2(row[0], iota_win, tab[0])
+        some(numbers_s, 1)
         for i, step in enumerate(STEPS):
             if step == "P":
                 pick2(V("wi", 0, C) if i == len(STEPS) - 1 else row[1], row[0], tab[0])
-                some(spare or spare2, 1)
+                some(spare, 1)
                 if i == 6:
                     for b in range(4): mm(b, 0, C, *E(b), V("qp"), V("sp"), True, False)
                     for b in range(4): mm(b, 0, C, *E(b), V("lc%d" % n), V("lp%d" % n), False, True)
-                row.reverse()
-                continue
-            if step == "F": pick("s", row[1], row[0], tab[0], HELP, C)
             else:
-                some(numbers, 2 if step == "T" else 0)
-                some(sums, int(step[1:] or 0))
-            diag(V("scan"), row[0])
-            if step == "F":
-                if HELP: pick("v", row[1], row[0], tab[0], 0, HELP)
-                row.reverse()
-            table(tab[1], V("scan"))
-            tab.reverse()
-            some(spare2, 1)
+                pick("s", row[1], row[0], tab[0], HELP, C)
+                diag(V("scan"), row[0])
+                pick("v", row[1], row[0], tab[0], 0, HELP)
+                table(tab[1], V("scan"))
+                tab.reverse()
+            some(numbers_s, 1)
+            if i >= SV0: some(sums_v, 1)
+            if i >= SS0: some(sums_s, 1)
+            row.reverse()
         pick2(V("arow"), V("wi"), V("fin"))
-        some(numbers)
-        some(spare2)
-        some(sums)
+        some(numbers_s)
+        some(sums_v)
+        some(sums_s)
         diag(V("scan"), V("arow"))
         at = V("atab")
         table(at, V("scan"))
         for b in range(3): pick("s", bit_of("zt", b), col("gs", b), at)
         lay(V("ainv"), at, iota_win)
-        pick("v", bit_of("zt", 3), col("gs", 3), at)
-        quant2("qz", "sz", 0, "zt")
-        mm(4, 0, B, *W(0), V("qz", 0, B), V("sz", 0, B))
-        mm(0, 0, C - B, *W(0), V("qz", B, C), V("sz", B, C))
+        for a, e in ((0, B), (B, C)): pick("v", bit_of("zt", 3), col("gs", 3), at, a, e)
+        thirds = [((4, 0, 1)[i], 128 * i, 128 * i + 128) for i in range(3)]
+        quant2("qz", "sz", 0, "zt", [t[1:] for t in thirds])
+        for bank, a, e in thirds: mm(bank, 0, 128, *W(0), V("qz", a, e), V("sz", a, e))
         for b in CORD: mm(4 + b, 0, C, *W(b), V("qz"), V("sz"))
         by_s = BACK_S.split()
-        for b in (3, 2, 1):
-            if any(w[0] == str(b) for w in by_s): mm(b, 0, C, *E(b), qx, sx)
         pick("s", V("ginv"), V("ainv"), invf)
         pick("s", col("frow", nxt), frow, at, 0, RH)
         diag(V("isc"), V("ginv"))
-        ts(V("pc", 0, B), V("ps4", 0, B), 2.0 ** -6, OP.mult)
+        ts(V("pc", 0, 128), V("ps4", 0, 128), 2.0 ** -6, OP.mult)
         table(invr, V("isc"))
         if n == 1: quant(V("vq"), V("vs"), V("vt"))
-        act(V("pc", B, C), V("ps0", 0, C - B), scale=2.0 ** -6)
+        for bank, a, e in thirds[1:]: act(V("pc", a, e), V("ps%d" % bank, 0, 128), scale=2.0 ** -6)
+        for b in (3, 2, 1):
+            if any(w[0] == str(b) for w in by_s): mm(b, 0, C, *E(b), qx, sx)
         for b in CORD: act(col("pc", b), V("ps%d" % (4 + b), 0, C), scale=2.0 ** -6)
         piece = {"A": (0, B), "B": (B, C), "C": (0, C)}
         for w in by_s:
             if w == "R": pick("s", col("frow", nxt), frow, at, RH, C)
             else: pick("s", col("p3", int(w[0])), col("pc", int(w[0])), invr, *piece[w[1]])
+        if n == 2:
+            do("s", lambda: g.scalar.activation(T.lnf[:, :], ap(col("frow", 1)), ACT.Identity, bias=float(MID)), [col("frow", 1)], [V("lnf")])
         for w in (BACK_V if n < 2 else LAST_V).split():
             if w == "r":
                 diag(V("rsc"), col("frow", nxt))
@@ -355,10 +351,9 @@ def rank_program(g, core, T, topo):
                     store("y", T.oc[:, 4 * a:4 * e], q, "oc%d" % k, codes=True)
                     mm(4 + k, 0, e - a, V("vq"), V("vs"), q, s)
                     if k == 0:
+                        store("y", T.ln[:, :], V("lnf"), "ol", a=T.lnf[0:128:16, :])
                         act(V("ysb", a, e), V("ps4", 0, e - a))
                         store("s", T.y[:, a:e], V("ysb", a, e), "oy0")
-                        do("s", lambda: g.scalar.activation(T.lnf[:, :], ap(col("frow", 1)), ACT.Identity, bias=float(MID)), [col("frow", 1)], [V("lnf")])
-                        store("s", T.ln[:, :], V("lnf"), "ol", a=T.lnf[0:128:16, :])
                 elif k == 0:
                     mm(4, 0, B, V("urq"), V("urs"), q, s)
                     act(V("brow", 0, B), V("ps4", 0, B), func=ACT.Sign)

from concourse.mybir import dt, AluOpType as OP, ActivationFunctionType as ACT

C = 384
K = C // 16
H = 192
B = 256
MASKS = (1, 2, 3)
MID = 192
BIG = 2.0 ** 22

SCRATCH = {}
def _buffers(where, kind, **widths):
    for name, width in widths.items(): SCRATCH[name] = (where, [128, width], kind)
_buffers("sbuf", "bfloat16", wi=2 * C, m16=16, msk=C, eb0=520, eb=520, ut=512, vt=512, xt=4 * C, xp=4 * C, zt=4 * C, fh=3 * C,
         brow=C, bsc=C, msg=6 * K, row=2 * C, scan=C, arow=C, ainv=C, ginv=C, isc=C, frow=2 * C, rsc=C, lb0=2 * K, lb1=2 * K, lb2=2 * K)
_buffers("sbuf", "int32", dmod=16, dmod2=16, pt=K, pt2=K, st=K, ui=8, fl32=K)
_buffers("sbuf", "float32", m1=16, m2=16, cc=K, ca=K, cb=K, scc=8, gs=4 * C, pc=4 * C, p3=4 * C, w1=2 * K, w2=2 * K, w3=K, w4=K, w5=K, t1=2 * K, t2=2 * K,
         fq=3 * K, le0=K, le1=K, le2=K, lnf=C, ysb=C)
_buffers("sbuf", "uint16", poff=K, uoff=8, tab=2 * K, fin=K, atab=K, inv=2 * K, ftab=K, f4=4 * K)
_buffers("sbuf", "float8_e4m3fn_x4", ebq=512, uq=128, urq=128, vq=128, wq=512, qx=4 * C, qp=C, qz=C, lc0=C, lc1=C, lc2=C)
_buffers("sbuf", "uint8", ebs=512, us=128, urs=128, vs=128, wss=512, sx=4 * C, sp=C, sz=C, lp0=C, lp1=C, lp2=C)
_buffers("psum", "float32", ps0=512, ps1=512, ps2=512, ps3=512, ps4=512, ps5=512, ps6=512, ps7=512)

SEMAPHORES = ["cv", "cs", "ct", "cg", "sent"]
SEMAPHORES += ["%s%d" % (_k, _n) for _k in ("ae", "ab", "ac", "ap") for _n in range(3)]
SEMAPHORES += ["dx", "dx2", "du", "dv", "df", "dw", "dws", "oy0", "oy1", "ol", "oc0", "oc1", "os0", "os1", "os2", "os3"]

STEPS = ["P", "F"] * 6 + ["P"]
HELP = 128
OWN = ((0, 0), (3, 0))
XP_S = 3
BACK_V = "0C 1C 2A 3A 2B qA 3B r qB"
LAST_V = "0A 1A 2A 3A qA 0B 1B 2B 3B qB"
BACK_S = "3A 3B R"
CORD = (1, 3, 2)
RH = 128
SV0 = 10
SS0 = 11
G1 = 4
G2 = 1


def rank_program(g, core, T, topo):
    rank = T.rank_of(core)
    if rank is None:
        return
    queue = {"v": g.vector, "s": g.scalar, "t": g.tensor, "g": g, "y": g.sync}
    counter = {"v": "cv", "s": "cs", "t": "ct", "g": "cg"}
    total = {}
    known = {q: {} for q in queue}
    clock = {}
    book = {}

    def wait(q, tok):
        k = known[q]
        if k.get(tok[0], 0) < tok[1]:
            queue[q].wait_ge(T.sem[tok[0]], tok[1])
            for s, v in list(clock.get(tok, {}).items()) + [tok]:
                if k.get(s, 0) < v: k[s] = v

    def meets(x, y):
        if max(x[0], y[0]) >= min(x[1], y[1]): return False
        return not (x[2] == y[2] > 1 and (x[0] - y[0]) % x[2])

    def covers(x, y):
        return x[0] <= y[0] and y[1] <= x[1] and (x[2] == 1 or (x[2] == y[2] and (x[0] - y[0]) % x[2] == 0))

    def span(v):
        return (0, 512, 1) if v[0][:2] == "ps" else v[1:]

    def need(q, rd, wr, joins=False):
        toks = {}
        for v in rd + wr:
            w = v in wr or v[0][:2] == "ps"
            for isw, s, tok in book.get(v[0], []):
                own = tok[0] == counter.get(q)
                if own and v[0][:2] == "ps" and v not in wr: continue
                if (w or isw) and meets(span(v), s) and not (joins and v in wr and own):
                    toks[tok[0]] = max(toks.get(tok[0], 0), tok[1])
        for s in sorted(toks, key=lambda s: s in ("cv", "cs", "ct", "cg")):
            wait(q, (s, toks[s]))

    def note(rd, wr, tok):
        for v in wr + rd:
            w = v in wr or v[0][:2] == "ps"
            b = book.setdefault(v[0], [])
            if w: b[:] = [r for r in b if not covers(span(v), r[1])]
            b.append((w, span(v), tok))

    def do(q, call, rd, wr, joins=False, sem=None, n=1):
        need(q, rd, wr, joins)
        s = sem or counter[q]
        total[s] = total.get(s, 0) + n
        tok = (s, total[s])
        call().then_inc(T.sem[s], n)
        clock[tok] = dict(known[q])
        note(rd, wr, tok)

    def V(name, a=0, b=None, step=1):
        return (name, a, SCRATCH[name][1][1] if b is None else b, step)

    def ap(v):
        n, a, b, st = v
        return T[n][:, a:b] if st == 1 else T[n][:, a:b:st]

    def part(v, a, b):
        return (v[0], v[1] + a * v[3], min(v[2], v[1] + b * v[3]), v[3])

    def load(q, out, src, sem, codes=False):
        dst = ap(out).bitcast(dt.uint8) if codes else ap(out)
        do(q, lambda: queue[q].dma_start(dst, src), [], [out], sem=sem, n=16)

    def store(q, dst, in_, sem, codes=False, a=None):
        src = a if a is not None else (ap(in_).bitcast(dt.uint8) if codes else ap(in_))
        do(q, lambda: queue[q].dma_start(dst, src), [in_], [], sem=sem, n=16)

    def fill(out, value):
        do("v", lambda: g.vector.memset(ap(out), value), [], [out])

    def copy(out, in_):
        do("v", lambda: g.vector.tensor_copy(ap(out), ap(in_)), [in_], [out])

    def act(out, in_, scale=1.0, func=ACT.Copy):
        do("s", lambda: g.scalar.activation(ap(out), ap(in_), func, scale=scale), [in_], [out])

    def ts(out, in_, s1, op0, s2=None, op1=None, extra=()):
        if op1 is None: do("v", lambda: g.vector.tensor_scalar(ap(out), ap(in_), s1, None, op0), [in_] + list(extra), [out])
        else: do("v", lambda: g.vector.tensor_scalar(ap(out), ap(in_), s1, s2, op0, op1), [in_] + list(extra), [out])

    def tt(out, a, b, op):
        do("v", lambda: g.vector.tensor_tensor(ap(out), ap(a), ap(b), op), [a, b], [out])

    def scan(out, d0, d1, first=0.0, op0=OP.mult):
        do("v", lambda: g.vector.tensor_tensor_scan(ap(out), ap(d0), ap(d1), first, op0, OP.add), [d0, d1], [out])

    def pick(q, out, win, off, a=0, b=C):
        out, off = part(out, a, b), part(off, a // 16, b // 16)
        if q == "v": do("v", lambda: g.vector.tensor_copy(ap(out), ap(win).indirect(ap(off))), [win, off], [out])
        else: do("s", lambda: g.scalar.activation(ap(out), ap(win).indirect(ap(off)), ACT.Copy), [win, off], [out])

    def pickadd(out, win, off, other, a=0, b=C):
        out, off, other = part(out, a, b), part(off, a // 16, b // 16), part(other, a, b)
        do("v", lambda: g.vector.tensor_tensor(ap(out), ap(win).indirect(ap(off)), ap(other), OP.add), [win, off, other], [out])

    def lay(win, off, in_):
        do("v", lambda: g.vector.tensor_copy(ap(win).indirect(ap(off)), ap(in_)), [in_, off], [win])

    def quant(q, s, t):
        do("v", lambda: g.vector.quantize_mx(ap(q), ap(s), ap(t)), [t], [q, s])

    def quant2(q, s, at, t, pieces=((0, B), (B, C))):
        for a, b in pieces: quant(V(q, at + a, at + b), V(s, at + a, at + b), V(t, 4 * a, 4 * b))

    def mm(bank, a, b, wq, ws, xq, xs, start=True, stop=True):
        out = V("ps%d" % bank, a, b)
        do("t", lambda: g.tensor.matmul_mx(ap(out), ap(wq), ap(ws), ap(xq), ap(xs), start, stop), [wq, ws, xq, xs], [out], joins=not start)

    def diag(sc, row, a=0, b=C):
        scan(part(sc, a, b), V("msk", a, b), part(row, a, b))

    def table(out, sc, mul=0, add=MID + 0.25):
        ts(out, V(sc[0], 15, C, 16), T.scc[:, mul:mul + 1], OP.mult, add, OP.add, extra=[V("scc")])

    def pick2(out, win, off):
        pick("s", out, win, off, H, C)
        pick("v", out, win, off, 0, H)

    def send(dst, out, in_, sem, codes=False):
        need("g", [in_], [])
        rid, pid, _e = topo.addr(dst)
        o, i = (ap(out).bitcast(dt.uint8), ap(in_).bitcast(dt.uint8)) if codes else (ap(out), ap(in_))
        g.remote_dma(o, i, T.sem[sem], T.sem["sent"], pid, rid, topo.mask(core, dst))
        total["sent"] = total.get("sent", 0) + len(topo.engines(core, dst))

    def arrives(name, sem, src):
        tok = (sem, len(topo.engines(src, core)))
        total[sem] = tok[1]
        note([], [V(name)], tok)

    def col(name, n, width=C): return V(name, width * n, width * n + width)
    def E(b): return col("ebq", b, 128), col("ebs", b, 128)
    def W(b): return col("wq", b, 128), col("wss", b, 128)
    def bit_of(name, b): return V(name, b, 4 * C, 4)
    def even(name): return V(name, 0, 2 * K, 2)
    def odd(name): return V(name, 1, 2 * K, 2)
    def some(calls, k=99):
        for call in calls[:k]: call()
        del calls[:k]

    partner = [T.cores[rank ^ m] for m in MASKS]
    iota_win = V("wi", C, 2 * C)
    for n in range(3):
        for k, s in (("le", "ae"), ("lb", "ab"), ("lc", "ac"), ("lp", "ap")):
            arrives("%s%d" % (k, n), "%s%d" % (s, n), partner[n])

    load("s", V("fl32"), T.fl[:, :], "df")
    load("y", V("ut"), T.u[:, :], "du")
    load("y", V("xt", 0, 4 * B), T.x[:, 0:4 * B], "dx")
    load("y", V("xt", 4 * B, 4 * C), T.x[:, 4 * B:4 * C], "dx2")
    need("y", [V("lp0")], [])
    load("y", V("wq"), T.wc[:, :], "dw", codes=True)
    load("y", V("wss"), T.ws[:, :], "dws")
    load("y", V("vt"), T.v[:, :], "dv")

    def iota(out, pattern, base, cm):
        do("g", lambda: g.iota(ap(out), pattern, base, cm, allow_small_or_imprecise_dtypes=True), [], [out])
    fill(V("eb0"), 0.5)
    iota(V("dmod"), [[1, 16]], 0, -1)
    iota(V("pt"), [[0, K]], 0, 1)
    iota(V("ui"), [[16, 8]], 0, 0)
    iota(V("st"), [[16, K]], 0, 0)
    do("g", lambda: g.affine_select(T.eb[:, :], T.eb0[:, :], [[1, 520]], OP.is_equal, 0.0, -4, -4), [V("eb0")], [V("eb")])
    fill(V("msg"), 0.0)
    ts(V("dmod2"), V("dmod"), 15, OP.bitwise_and)
    scan(iota_win, V("eb0", 0, C), V("eb0", 0, C), -MID - 1.0, OP.add)
    ts(V("pt2"), V("pt"), 15, OP.bitwise_and)
    ts(V("m1"), V("dmod2"), 1.0, OP.is_equal, BIG - 1.0, OP.mult)
    ts(V("m2"), V("dmod2"), 0.0, OP.not_equal)
    copy(V("uoff"), V("ui"))
    copy(V("poff"), V("pt2"))
    ts(V("scc", 7, 8), V("pt2", 0, 1), 15.0, OP.is_equal)
    tt(V("m16"), V("m1"), V("m2"), OP.add)
    pick("s", V("msk"), V("m16"), V("poff"))
    tt(V("cc"), V("pt2"), V("st"), OP.add)
    for i, (last, others) in enumerate(((1.0, 1.0 / BIG), (4.0, 4.0 / BIG), (0.5, 0.5 * BIG), (0.25, 0.25 / BIG))):
        ts(V("scc", i, i + 1), V("scc", 7, 8), last - others, OP.mult, others, OP.add)
    ts(V("ca"), V("cc"), 0.25, OP.mult)
    ts(V("cb"), V("cc"), 0.25, OP.mult, 0.25 * C, OP.add)
    ts(col("fq", 0, K), V("fl32"), 0.25, OP.mult)
    send(partner[0], V("le0"), col("fq", 0, K), "ae0")
    copy(V("ftab"), V("fl32"))
    four = [lambda b=b: ts(col("f4", b, K), V("fl32"), 4.0, OP.mult, float(b), OP.add) for b in range(4)]
    some(four, 1)
    quant(V("uq"), V("us"), V("ut"))
    some(four)
    do("v", lambda: g.vector.tensor_copy(T.urq[:, :].bitcast(dt.uint32), T.uq[:, :].bitcast(dt.uint32).indirect(T.uoff[:, 0:8])), [V("uq"), V("uoff")], [V("urq")])
    pick("s", V("urs"), V("us"), V("uoff"), 0, 128)
    pick("s", col("frow", 0), iota_win, V("ftab"))

    for n in range(3):
        qx, sx = col("qx", n), col("sx", n)
        cur, nxt = n % 2, (n + 1) % 2
        frow, invf, invr = col("frow", cur), col("inv", cur, K), col("inv", nxt, K)
        msg = col("msg", n, 2 * K)
        bt = V("msg", msg[1] + 1, msg[2], 2)
        if n:
            gaps = [lambda: table(col("fq", n, K), V("rsc"), 3, 0.25 * MID), lambda: send(partner[n], V("le%d" % n), col("fq", n, K), "ae%d" % n)]
            gaps += [lambda b=b: table(col("f4", b, K), V("rsc"), 1, 4.0 * MID + b + 0.25) for b in range(4)]
        else:
            gaps = [lambda b=b: quant(*E(b), V("eb", 4 - b, 516 - b)) for b in range(4)]
            quant2("qx", "sx", 0, "xt")
            mm(4, 0, B, V("urq"), V("urs"), part(qx, 0, B), part(sx, 0, B))
            act(V("brow", 0, B), V("ps4", 0, B), func=ACT.Sign)
        mm(5, 0, C - B, V("urq"), V("urs"), part(qx, B, C), part(sx, B, C))
        act(V("brow", B, C), V("ps5", 0, C - B), func=ACT.Sign)
        some(gaps, G1)
        diag(V("bsc"), V("brow"), 0, B)
        some(gaps, G2)
        diag(V("bsc"), V("brow"), B, C)
        some(gaps)
        ts(bt, V("bsc", 15, C, 16), T.scc[:, 2:3], OP.is_gt, 0.5, OP.subtract, extra=[V("scc")])
        send(partner[n], V("lb%d" % n), msg, "ab%d" % n)
        send(partner[n], V("lc%d" % n), qx, "ac%d" % n, codes=True)
        send(partner[n], V("lp%d" % n), sx, "ap%d" % n)
        for b in range(3): mm(4 + b, 0, C, *E(b), qx, sx)
        def out_of(call, out, bank, count, w):
            return [lambda b=b, a=a: call(V(out, C * b + a, C * b + a + w), V("ps%d" % (bank + b), a, a + w)) for b in range(count) for a in range(0, C, w)]
        own_v, own_s = OWN[min(n, 1)]
        numbers_v, numbers_s = out_of(copy, "fh", 4, 3, 128)[:own_v], out_of(act, "fh", 4, 3, 128)[own_v:]
        sums_v, sums_s = out_of(copy, "gs", 0, 2, H), out_of(act, "gs", 0, 4, 128)[6:]
        xs = XP_S if n else 4
        for b in range(4): pick("s" if b < xs else "v", bit_of("xp", b), V("xt"), col("f4", b, K))
        if n == 0: lay(V("ainv"), V("ftab"), iota_win)
        some(numbers_v)
        some(numbers_s, own_s)
        le = V("le%d" % n)
        ts(V("w5"), bt, 4.0, OP.mult)
        tt(V("w3"), le, V("ca"), OP.subtract)
        tt(V("w4"), V("cb"), le, OP.subtract)
        tt(odd("w1"), le, V("ca"), OP.add)
        tt(odd("w2"), le, V("cb"), OP.add)
        tt(even("w1"), V("w3"), V("w5"), OP.mult)
        tt(even("w2"), V("w4"), V("w5"), OP.mult)
        spare = [lambda a=a: quant2("qp", "sp", 0, "xp", [(a, a + 128)]) for a in (0, 128, 256)]
        if n == 0: spare += [lambda: diag(V("isc"), V("ainv")), lambda: table(invf, V("isc"))]
        scan(V("t1"), V("lb%d" % n), V("w1"))
        scan(V("t2"), V("lb%d" % n), V("w2"))
        tab, row = [col("tab", i, K) for i in range(2)], [col("row", i) for i in range(2)]
        ts(tab[0], odd("t1"), 2.0, OP.mult, 0.25, OP.add)
        ts(V("fin"), odd("t2"), 2.0, OP.mult, 0.25, OP.add)
        pick2(row[0], iota_win, tab[0])
        some(numbers_s, 1)
        for i, step in enumerate(STEPS):
            if step == "P":
                pick2(V("wi", 0, C) if i == len(STEPS) - 1 else row[1], row[0], tab[0])
                some(spare, 1)
                if i == 6:
                    for b in range(4): mm(b, 0, C, *E(b), V("qp"), V("sp"), True, False)
                    for b in range(4): mm(b, 0, C, *E(b), V("lc%d" % n), V("lp%d" % n), False, True)
            else:
                pick("s", row[1], row[0], tab[0], HELP, C)
                diag(V("scan"), row[0])
                pick("v", row[1], row[0], tab[0], 0, HELP)
                table(tab[1], V("scan"))
                tab.reverse()
            some(numbers_s, 1)
            if i >= SV0: some(sums_v, 1)
            if i >= SS0: some(sums_s, 1)
            row.reverse()
        pick2(V("arow"), V("wi"), V("fin"))
        some(numbers_s)
        some(sums_v)
        some(sums_s)
        diag(V("scan"), V("arow"))
        at = V("atab")
        table(at, V("scan"))
        for b in range(3): pick("s", bit_of("zt", b), col("gs", b), at)
        lay(V("ainv"), at, iota_win)
        for a, e in ((0, B), (B, C)): pick("v", bit_of("zt", 3), col("gs", 3), at, a, e)
        thirds = [((4, 0, 1)[i], 128 * i, 128 * i + 128) for i in range(3)]
        quant2("qz", "sz", 0, "zt", [t[1:] for t in thirds])
        for bank, a, e in thirds: mm(bank, 0, 128, *W(0), V("qz", a, e), V("sz", a, e))
        for b in CORD: mm(4 + b, 0, C, *W(b), V("qz"), V("sz"))
        by_s = BACK_S.split()
        pick("s", V("ginv"), V("ainv"), invf)
        pick("s", col("frow", nxt), frow, at, 0, RH)
        diag(V("isc"), V("ginv"))
        ts(V("pc", 0, 128), V("ps4", 0, 128), 2.0 ** -6, OP.mult)
        table(invr, V("isc"))
        if n == 1: quant(V("vq"), V("vs"), V("vt"))
        for bank, a, e in thirds[1:]: act(V("pc", a, e), V("ps%d" % bank, 0, 128), scale=2.0 ** -6)
        for b in (3, 2, 1):
            if any(w[0] == str(b) for w in by_s): mm(b, 0, C, *E(b), qx, sx)
        for b in CORD: act(col("pc", b), V("ps%d" % (4 + b), 0, C), scale=2.0 ** -6)
        piece = {"A": (0, B), "B": (B, C), "C": (0, C)}
        for w in by_s:
            if w == "R": pick("s", col("frow", nxt), frow, at, RH, C)
            else: pick("s", col("p3", int(w[0])), col("pc", int(w[0])), invr, *piece[w[1]])
        if n == 2:
            do("s", lambda: g.scalar.activation(T.lnf[:, :], ap(col("frow", 1)), ACT.Identity, bias=float(MID)), [col("frow", 1)], [V("lnf")])
        for w in (BACK_V if n < 2 else LAST_V).split():
            if w == "r":
                diag(V("rsc"), col("frow", nxt))
                continue
            a, e = piece[w[1]]
            if w[0] == "q":
                q, s = part(col("qx", n + 1), a, e), part(col("sx", n + 1), a, e)
                quant(q, s, V("xt", 4 * a, 4 * e))
                k = int(w[1] == "B")
                if n == 2:
                    store("y", T.oc[:, 4 * a:4 * e], q, "oc%d" % k, codes=True)
                    mm(4 + k, 0, e - a, V("vq"), V("vs"), q, s)
                    if k == 0:
                        store("y", T.ln[:, :], V("lnf"), "ol", a=T.lnf[0:128:16, :])
                        act(V("ysb", a, e), V("ps4", 0, e - a))
                        store("s", T.y[:, a:e], V("ysb", a, e), "oy0")
                elif k == 0:
                    mm(4, 0, B, V("urq"), V("urs"), q, s)
                    act(V("brow", 0, B), V("ps4", 0, B), func=ACT.Sign)
                continue
            b = int(w[0])
            if w in by_s or w[0] + "C" in by_s: tt(part(bit_of("xt", b), a, e), V("ps%d" % b, a, e), part(col("p3", b), a, e), OP.add)
            else: pickadd(bit_of("xt", b), col("pc", b), invr, col("fh", b), a, e)
    for k in range(4):
        store("y" if k < 2 else "s", T.osc[4 * k:4 * k + 4, :], col("sx", 3), "os%d" % k, a=T.sx[32 * k:32 * k + 4, 3 * C:4 * C])
    copy(V("ysb", B, C), V("ps5", 0, C - B))
    store("y", T.y[:, B:C], V("ysb", B, C), "oy1")
    for s in sorted(total):
        wait("g", (s, total[s]))
